import numpy as np
import ml_dtypes


def mxq(x, axis, fmt="e4m3"):
    dtype, down = {"e4m3": (ml_dtypes.float8_e4m3fn, 7), "e5m2": (ml_dtypes.float8_e5m2, 14)}[fmt]
    v = np.moveaxis(np.asarray(x, np.float32).astype(ml_dtypes.bfloat16).astype(np.float64), axis, -1)
    blocks = v.reshape(v.shape[:-1] + (-1, 32))
    amax = np.abs(blocks).max(-1, keepdims=True)
    byte = np.maximum(np.where(amax > 0, np.frexp(amax)[1] - 1 + 127, 0) - down, 1)
    scale = np.exp2(byte - 127.0)
    codes = (blocks / scale).astype(np.float32).astype(dtype).astype(np.float64)
    return np.moveaxis((codes * scale).reshape(v.shape), -1, axis)


WIDE = False


def mx_kscale(k):
    if not WIDE:
        return np.ones(k)
    levels = np.array([10, -10, 5, -5, 0])
    if k % 512:
        return np.exp2(np.random.permutation(np.resize(levels, k // 32))).repeat(32)
    a = np.empty((k // 512, 16))
    for p in range(k // 512):
        a[p, :8] = np.random.permutation(np.resize(levels, 8))
        for g in range(8):
            far = levels[np.abs(levels - a[p, g]) >= 10]
            a[p, g + 8] = far[np.random.randint(len(far))]
    return np.exp2(a.ravel()).repeat(32)


def f64(x):
    return np.asarray(x).astype(np.float64)


def striped(idx):
    return np.tile(idx.reshape(-1, 16).T, (8, 1)).astype(np.uint16)


def unstriped(offs):
    return offs[:16].T.reshape(-1).astype(np.int64)


def pack_weight(w):
    k, n = w.shape
    w = f64(np.asarray(w, np.float32).astype(ml_dtypes.bfloat16)).reshape(k // 32, 32, n)
    amax = np.abs(w).max(1)
    byte = np.clip(np.where(amax > 0, np.frexp(amax)[1] - 1 + 127 - 7, 1), 1, 254)
    scaled = (w * np.exp2(127.0 - byte)[:, None, :]).reshape(k, n).astype(np.float32)
    words = np.ascontiguousarray(scaled.reshape(k // 512, 128, 4, n).transpose(0, 1, 3, 2)).astype(ml_dtypes.float8_e4m3fn).view(np.uint8)
    return words, np.ascontiguousarray(byte.astype(np.uint8).reshape(k // 512, 16, n))


def unpack_weight(words, scales):
    g, p, n, _ = words.shape
    vals = np.ascontiguousarray(words).view(ml_dtypes.float8_e4m3fn).astype(np.float64) * np.repeat(np.exp2(scales.astype(np.float64) - 127.0), 8, axis=1)[..., None]
    return vals.transpose(0, 1, 3, 2).reshape(g * 512, n)


E2M1 = np.array([0.0, 0.5, 1.0, 1.5, 2.0, 3.0, 4.0, 6.0, -0.0, -0.5, -1.0, -1.5, -2.0, -3.0, -4.0, -6.0])


def pack_fp4(w):
    k, n = w.shape
    w = f64(np.asarray(w, np.float32).astype(ml_dtypes.bfloat16)).reshape(k // 32, 32, n)
    amax = np.abs(w).max(1)
    mant, ex = np.frexp(amax / 6.0)
    byte = np.clip(np.where(amax > 0, np.where(mant > 0.5, ex, ex - 1) + 127, 1), 1, 254)
    scaled = (w * np.exp2(127.0 - byte)[:, None, :]).reshape(k, n).astype(np.float32)
    c = np.ascontiguousarray(scaled.reshape(k // 512, 128, 4, n).transpose(0, 1, 3, 2)).astype(ml_dtypes.float4_e2m1fn).view(np.uint8) & 0xF
    words = (c[..., 0::2] | (c[..., 1::2] << 4)).reshape(k // 512, 128, 2 * n)
    return np.ascontiguousarray(words), np.ascontiguousarray(byte.astype(np.uint8).reshape(k // 512, 16, n))


def unpack_fp4(words, scales):
    g, _, n = scales.shape
    words = np.ascontiguousarray(words).reshape(g, 128, n, 2)
    nib = np.empty((g, 128, n, 4), np.uint8)
    nib[..., 0::2] = words & 0xF
    nib[..., 1::2] = words >> 4
    vals = E2M1[nib] * np.repeat(np.exp2(scales.astype(np.float64) - 127.0), 8, axis=1)[..., None]
    return vals.transpose(0, 1, 3, 2).reshape(g * 512, n)


def planes(y):
    n, m = y.shape
    v = y.astype(np.float32).astype(ml_dtypes.bfloat16).astype(np.float64).reshape(n // 32, 32, m)
    top = np.abs(v).max(1)
    byte = np.clip(np.where(top > 0, np.frexp(top)[1] - 1 + 127 - 7, 1), 1, 254)
    codes = (v * np.exp2(127.0 - byte)[:, None, :]).reshape(n, m).astype(np.float32).astype(ml_dtypes.float8_e4m3fn).view(np.uint8)
    words = codes.reshape(n // 512, 128, 4, m).transpose(0, 1, 3, 2)
    return np.ascontiguousarray(words), np.ascontiguousarray(byte.astype(np.uint8).reshape(n // 512, 16, m))


def relu(v):
    return np.maximum(v, 0.0)


K, T, S, H, N = 1024, 1024, 512, 512, 512


def setup_inputs():
    n = np.random.standard_normal
    s = mx_kscale(K)[:, None]
    u = mx_kscale(H)
    packed_xT = pack_weight(n((K, T)) * s)
    packed_w2 = pack_fp4(n((H, N)) / np.sqrt(2 * H) / u[:, None])
    packed_w3 = pack_fp4(n((K, N)) / np.sqrt(2 * K) / s)
    return {
        "x_words": packed_xT[0],
        "x_scales": packed_xT[1],
        "w1": (n((K, H)) / np.sqrt(K) / s * u).astype(np.float32),
        "w2_words": packed_w2[0],
        "w2_scales": packed_w2[1],
        "w3_words": packed_w3[0],
        "w3_scales": packed_w3[1],
        "offs": striped(np.random.permutation(T)[:S]),
    }


def reference(x_words, x_scales, w1, w2_words, w2_scales, w3_words, w3_scales, offs):
    xq = unpack_weight(x_words, x_scales)[:, unstriped(offs)]
    h = relu(mxq(f64(w1), 0, "e4m3").T @ xq)
    out_0 = unpack_fp4(w2_words, w2_scales).T @ mxq(h, 0, "e4m3") + unpack_fp4(w3_words, w3_scales).T @ xq
    return (out_0,) + planes(out_0)

@@ -1,0 +1,216 @@
+from contextlib import ExitStack
+
+import concourse.mybir as mybir
+
+K, T, S, H, N = 1024, 1024, 512, 512, 512
+FLOPS = 2 * S * (K * H + H * N + K * N)
+
+F32 = mybir.dt.float32
+BF16 = mybir.dt.bfloat16
+I32 = mybir.dt.int32
+U32 = mybir.dt.uint32
+U16 = mybir.dt.uint16
+U8 = mybir.dt.uint8
+FP8X4 = mybir.dt.float8_e4m3fn_x4
+FP4X4 = mybir.dt.float4_e2m1fn_x4
+ACT = mybir.ActivationFunctionType
+
+P = 128
+PACK = 4
+K_PASS = P * PACK
+PASSES = K // K_PASS
+CHUNK = 128
+CHUNKS = S // CHUNK
+HALF = H // 2
+
+
+def tile_picked_zskip_relu_po_kernel(
+    tc, x_words, x_scales, w1, w2_words, w2_scales, w3_words, w3_scales, offs, out_0, out_1, out_2
+):
+    nc = tc.nc
+    with ExitStack() as ctx:
+        sb = ctx.enter_context(tc.tile_pool(name="sb", bufs=1))
+        ps = ctx.enter_context(tc.psum_pool(name="ps", bufs=1))
+
+        def tile(shape, dtype, name):
+            return sb.tile(shape, dtype, name=name, align_bytes=64)
+
+        offsets = sb.tile([P, S // 16], U16, name="offsets")
+        xw = [tile([P, T], I32, f"xw{o}") for o in range(PASSES)]
+        xs = tile([P, T], U8, "xs")
+        xg = [tile([P, S], U32, f"xg{o}") for o in range(PASSES)]
+        xsg = tile([P, S], U8, "xsg")
+        xs1 = tile([P, S], U8, "xs1")
+        w3_raw = tile([P, PASSES, 2 * N], U8, "w3_raw")
+        w2_raw = tile([P, 2 * N], U8, "w2_raw")
+        w3s_raw = tile([P, PASSES, N], U8, "w3s_raw")
+        w2s_raw = tile([P, N], U8, "w2s_raw")
+        w3_d = tile([P, PASSES, 2 * N], U8, "w3_d")
+        w2_d = tile([P, 2 * N], U8, "w2_d")
+        w3s_d = tile([P, PASSES, N], U8, "w3s_d")
+        w2s_d = tile([P, N], U8, "w2s_d")
+        w1_raw = [[tile([P, PACK, HALF], F32, f"w1_raw{o}{u}") for u in range(2)] for o in range(PASSES)]
+        w1_bf = [tile([P, PACK, P, PACK], BF16, f"w1_bf{o}") for o in range(PASSES)]
+        w1_q = [tile([P, H], U32, f"w1_q{o}") for o in range(PASSES)]
+        w1_s = [tile([P, H], U8, f"w1_s{o}") for o in range(PASSES)]
+        h_bf = [tile([P, CHUNK, PACK], BF16, f"h_bf{c}") for c in range(CHUNKS)]
+        h_q = [tile([P, CHUNK], U32, f"h_q{c}") for c in range(CHUNKS)]
+        h_s = [tile([P, CHUNK], U8, f"h_s{c}") for c in range(CHUNKS)]
+        y = [tile([P, PACK, CHUNK], F32, f"y{c}") for c in range(CHUNKS)]
+        y_bf = [tile([P, CHUNK, PACK], BF16, f"y_bf{c}") for c in range(CHUNKS)]
+        y_q = tile([P, S], U32, "y_q")
+        y_s = tile([P, S], U8, "y_s")
+        zero = tile([P, 1], F32, "zero")
+        zero_bias = tile([P, 1], F32, "zero_bias")
+        h_ps = [ps.tile([P, PACK, CHUNK], F32, name=f"h_ps{c}") for c in range(CHUNKS)]
+        y_ps = [ps.tile([P, PACK, CHUNK], F32, name=f"y_ps{c}") for c in range(CHUNKS)]
+
+        nc.vector.memset(xs[:].bitcast(I32), 0)
+        nc.vector.memset(zero[:], 0.0)
+        nc.vector.memset(w3s_raw[:].rearrange("p o n -> p (o n)").bitcast(I32), 0)
+        nc.vector.memset(w2s_raw[:].bitcast(I32), 0)
+        nc.vector.memset(xs1[:].bitcast(I32), 0)
+        nc.scalar.activation(zero_bias[:], zero[:], ACT.Relu)
+
+        def load_x(o):
+            nc.sync.dma_start(xw[o][:], x_words[o].rearrange("p n t -> p (n t)").bitcast(I32))
+
+        def load_w1(o, u):
+            rows = w1[K_PASS * o : K_PASS * (o + 1), HALF * u : HALF * (u + 1)]
+            nc.sync.dma_start(w1_raw[o][u][:], rows.rearrange("(p j) c -> p j c", j=PACK))
+
+        nc.sync.dma_start(offsets[:], offs)
+        nc.sync.dma_start(w3_raw[:].bitcast(I32), w3_words.rearrange("o p n -> p o n").bitcast(I32))
+        load_x(0)
+        for q in range(4):
+            nc.sync.dma_start(xs[32 * q : 32 * q + 8, :].bitcast(I32), x_scales[:, 4 * q : 4 * q + 4, :].bitcast(I32))
+        nc.sync.dma_start(w2_raw[:].bitcast(I32), w2_words[0].bitcast(I32))
+        load_w1(0, 0)
+        for r in range(4):
+            nc.sync.dma_start(
+                w3s_raw[r:P:32, :, :].bitcast(I32), w3_scales[:, r:16:4, :].rearrange("o q n -> q o n").bitcast(I32)
+            )
+        load_w1(0, 1)
+        for r in range(4):
+            nc.sync.dma_start(w2s_raw[r:P:32, :].bitcast(I32), w2_scales[0, r:16:4, :].bitcast(I32))
+        load_w1(1, 0)
+        load_w1(1, 1)
+        load_x(1)
+
+        nc.vector.tensor_copy(
+            w3_d[:].rearrange("p o (t m b) -> p o t m b", t=PACK, b=2),
+            w3_raw[:].rearrange("p o (m t b) -> p o t m b", t=PACK, b=2),
+        )
+        nc.vector.tensor_copy(xsg[:], xs[:].indirect(offsets[:]))
+        for q in range(4):
+            nc.sync.dma_start(xs1[32 * q : 32 * q + 4, :].bitcast(I32), xsg[32 * q + 4 : 32 * q + 8, :].bitcast(I32))
+        nc.vector.tensor_copy(xg[0][:], xw[0][:].bitcast(U32).indirect(offsets[:]))
+        nc.vector.tensor_copy(
+            w3s_d[:].rearrange("p o (t m) -> p o t m", t=PACK),
+            w3s_raw[:].rearrange("p o (m t) -> p o t m", t=PACK),
+        )
+        nc.vector.tensor_copy(
+            w2_d[:].rearrange("p (t m b) -> p t m b", t=PACK, b=2),
+            w2_raw[:].rearrange("p (m t b) -> p t m b", t=PACK, b=2),
+        )
+        nc.vector.tensor_copy(
+            w2s_d[:].rearrange("p (t m) -> p t m", t=PACK),
+            w2s_raw[:].rearrange("p (m t) -> p t m", t=PACK),
+        )
+
+        def cast_w1(o, u):
+            dst = w1_bf[o][:, :, 64 * u : 64 * (u + 1), :].rearrange("p t m j -> p m t j")
+            src = w1_raw[o][u][:].rearrange("p j (m t) -> p m t j", t=PACK)
+            if (o, u) == (1, 1):
+                nc.vector.tensor_copy(dst, src)
+            else:
+                nc.scalar.activation(dst, src, ACT.Copy)
+
+        def quant_w1(o):
+            nc.vector.quantize_mx(
+                out=w1_q[o][:].bitcast(FP8X4), scales=w1_s[o][:], in_=w1_bf[o][:].rearrange("p t m j -> p (t m j)")
+            )
+
+        def cols(i):
+            return slice(P * i, P * (i + 1))
+
+        def mm1(o, c):
+            for t in range(PACK):
+                nc.tensor.matmul_mx(
+                    out=h_ps[c][:, t, :],
+                    lhsT=w1_q[o][:, cols(t)].bitcast(FP8X4),
+                    lhsT_scale=w1_s[o][:, cols(t)],
+                    rhs=xg[o][:, cols(c)].bitcast(FP8X4),
+                    rhs_scale=xsg[4 * o : P, cols(c)],
+                    start=(o == 0 and t == 0),
+                    stop=(o == PASSES - 1 and t == PACK - 1),
+                )
+
+        def mm3(o, c):
+            x_scale = xsg if o == 0 else xs1
+            for t in range(PACK):
+                nc.tensor.matmul_mx(
+                    out=y_ps[c][:, t, :],
+                    lhsT=w3_d[:, o, 256 * t : 256 * (t + 1)].bitcast(FP4X4),
+                    lhsT_scale=w3s_d[:, o, cols(t)],
+                    rhs=xg[o][:, cols(c)].bitcast(FP8X4),
+                    rhs_scale=x_scale[:, cols(c)],
+                    start=(o == 0 and t == 0),
+                    stop=False,
+                )
+
+        def mm2(c):
+            for t in range(PACK):
+                nc.tensor.matmul_mx(
+                    out=y_ps[c][:, t, :],
+                    lhsT=w2_d[:, 256 * t : 256 * (t + 1)].bitcast(FP4X4),
+                    lhsT_scale=w2s_d[:, cols(t)],
+                    rhs=h_q[c][:].bitcast(FP8X4),
+                    rhs_scale=h_s[c][:],
+                    start=False,
+                    stop=(t == PACK - 1),
+                )
+
+        for c in range(CHUNKS):
+            mm3(0, c)
+        cast_w1(0, 0)
+        cast_w1(0, 1)
+        quant_w1(0)
+        for c in range(CHUNKS):
+            mm1(0, c)
+        cast_w1(1, 0)
+        cast_w1(1, 1)
+        quant_w1(1)
+
+        for c in range(CHUNKS):
+            nc.vector.tensor_copy(xg[1][:, cols(c)], xw[1][:].bitcast(U32).indirect(offsets[:, 8 * c : 8 * (c + 1)]))
+        for c in range(CHUNKS):
+            mm1(1, c)
+            src = h_ps[c][:].rearrange("p t n -> p n t")
+            if c == 1:
+                nc.vector.tensor_scalar_max(h_bf[c][:], src, 0.0)
+            else:
+                nc.scalar.activation(h_bf[c][:], src, ACT.Relu, bias=zero_bias[:])
+            nc.vector.quantize_mx(
+                out=h_q[c][:].bitcast(FP8X4), scales=h_s[c][:], in_=h_bf[c][:].rearrange("p n t -> p (n t)")
+            )
+
+        out_rows = out_0.rearrange("(p t) n -> p t n", t=PACK)
+        out_words = out_1[0].rearrange("p n t -> p (n t)").bitcast(I32)
+        for c in range(CHUNKS):
+            mm3(1, c)
+            mm2(c)
+            nc.scalar.copy(y[c][:], y_ps[c][:])
+            nc.sync.dma_start(out_rows[:, :, cols(c)], y[c][:])
+            nc.vector.tensor_copy(
+                y_bf[c][:].rearrange("p (n i) t -> p n t i", i=4),
+                y[c][:].rearrange("p t (n i) -> p n t i", i=4),
+            )
+            nc.vector.quantize_mx(
+                out=y_q[:, cols(c)].bitcast(FP8X4),
+                scales=y_s[:, cols(c)],
+                in_=y_bf[c][:].rearrange("p n t -> p (n t)"),
+            )
+            nc.sync.dma_start(out_words[:, cols(c)], y_q[:, cols(c)].bitcast(I32))
+        for q in range(4):
+            nc.sync.dma_start(out_2[0, 4 * q : 4 * q + 4, :].bitcast(I32), y_s[32 * q : 32 * q + 4, :].bitcast(I32))

@@ -80,23 +80,28 @@ def tile_picked_zskip_relu_po_kernel(
             nc.sync.dma_start(w1_raw[o][u][:], rows.rearrange("(p j) c -> p j c", j=PACK))
 
         nc.sync.dma_start(offsets[:], offs)
+        nc.sync.dma_start(w2_raw[:].bitcast(I32), w2_words[0].bitcast(I32))
         nc.sync.dma_start(w3_raw[:].bitcast(I32), w3_words.rearrange("o p n -> p o n").bitcast(I32))
-        load_x(0)
         for q in range(4):
             nc.sync.dma_start(xs[32 * q : 32 * q + 8, :].bitcast(I32), x_scales[:, 4 * q : 4 * q + 4, :].bitcast(I32))
-        nc.sync.dma_start(w2_raw[:].bitcast(I32), w2_words[0].bitcast(I32))
+        load_x(0)
         load_w1(0, 0)
+        load_w1(1, 0)
         for r in range(4):
             nc.sync.dma_start(
                 w3s_raw[r:P:32, :, :].bitcast(I32), w3_scales[:, r:16:4, :].rearrange("o q n -> q o n").bitcast(I32)
             )
         load_w1(0, 1)
-        for r in range(4):
-            nc.sync.dma_start(w2s_raw[r:P:32, :].bitcast(I32), w2_scales[0, r:16:4, :].bitcast(I32))
-        load_w1(1, 0)
         load_w1(1, 1)
-        load_x(1)
+        for r in range(4):
+            if r == 3:
+                load_x(1)
+            nc.sync.dma_start(w2s_raw[r:P:32, :].bitcast(I32), w2_scales[0, r:16:4, :].bitcast(I32))
 
+        nc.vector.tensor_copy(
+            w2_d[:].rearrange("p (t m b) -> p t m b", t=PACK, b=2),
+            w2_raw[:].rearrange("p (m t b) -> p t m b", t=PACK, b=2),
+        )
         nc.vector.tensor_copy(
             w3_d[:].rearrange("p o (t m b) -> p o t m b", t=PACK, b=2),
             w3_raw[:].rearrange("p o (m t b) -> p o t m b", t=PACK, b=2),
@@ -109,19 +114,11 @@ def tile_picked_zskip_relu_po_kernel(
             w3s_d[:].rearrange("p o (t m) -> p o t m", t=PACK),
             w3s_raw[:].rearrange("p o (m t) -> p o t m", t=PACK),
         )
-        nc.vector.tensor_copy(
-            w2_d[:].rearrange("p (t m b) -> p t m b", t=PACK, b=2),
-            w2_raw[:].rearrange("p (m t b) -> p t m b", t=PACK, b=2),
-        )
-        nc.vector.tensor_copy(
-            w2s_d[:].rearrange("p (t m) -> p t m", t=PACK),
-            w2s_raw[:].rearrange("p (m t) -> p t m", t=PACK),
-        )
 
-        def cast_w1(o, u):
-            dst = w1_bf[o][:, :, 64 * u : 64 * (u + 1), :].rearrange("p t m j -> p m t j")
-            src = w1_raw[o][u][:].rearrange("p j (m t) -> p m t j", t=PACK)
-            if (o, u) == (1, 1):
+        def cast_w1(o, u, m0, m1, on_vector):
+            dst = w1_bf[o][:, :, 64 * u + m0 : 64 * u + m1, :].rearrange("p t m j -> p m t j")
+            src = w1_raw[o][u][:, :, PACK * m0 : PACK * m1].rearrange("p j (m t) -> p m t j", t=PACK)
+            if on_vector:
                 nc.vector.tensor_copy(dst, src)
             else:
                 nc.scalar.activation(dst, src, ACT.Copy)
@@ -173,17 +170,22 @@ def tile_picked_zskip_relu_po_kernel(
 
         for c in range(CHUNKS):
             mm3(0, c)
-        cast_w1(0, 0)
-        cast_w1(0, 1)
+        cast_w1(0, 0, 0, 64, False)
+        cast_w1(1, 0, 0, 64, False)
+        cast_w1(0, 1, 0, 64, True)
         quant_w1(0)
         for c in range(CHUNKS):
             mm1(0, c)
-        cast_w1(1, 0)
-        cast_w1(1, 1)
+        cast_w1(1, 1, 0, 40, False)
+        cast_w1(1, 1, 40, 64, True)
         quant_w1(1)
 
         for c in range(CHUNKS):
             nc.vector.tensor_copy(xg[1][:, cols(c)], xw[1][:].bitcast(U32).indirect(offsets[:, 8 * c : 8 * (c + 1)]))
+        nc.vector.tensor_copy(
+            w2s_d[:].rearrange("p (t m) -> p t m", t=PACK),
+            w2s_raw[:].rearrange("p (m t) -> p t m", t=PACK),
+        )
         for c in range(CHUNKS):
             mm1(1, c)
             src = h_ps[c][:].rearrange("p t n -> p n t")
@@ -200,17 +202,22 @@ def tile_picked_zskip_relu_po_kernel(
         for c in range(CHUNKS):
             mm3(1, c)
             mm2(c)
-            nc.scalar.copy(y[c][:], y_ps[c][:])
+            parts = [(0, CHUNK // 2), (CHUNK // 2, CHUNK)] if c == CHUNKS - 1 else [(0, CHUNK)]
+            for n0, n1 in parts:
+                nc.scalar.copy(y[c][:, :, n0:n1], y_ps[c][:, :, n0:n1])
             nc.sync.dma_start(out_rows[:, :, cols(c)], y[c][:])
-            nc.vector.tensor_copy(
-                y_bf[c][:].rearrange("p (n i) t -> p n t i", i=4),
-                y[c][:].rearrange("p t (n i) -> p n t i", i=4),
-            )
-            nc.vector.quantize_mx(
-                out=y_q[:, cols(c)].bitcast(FP8X4),
-                scales=y_s[:, cols(c)],
-                in_=y_bf[c][:].rearrange("p n t -> p (n t)"),
-            )
+            for n0, n1 in parts:
+                nc.vector.tensor_copy(
+                    y_bf[c][:, n0:n1, :].rearrange("p (n i) t -> p n t i", i=4),
+                    y[c][:, :, n0:n1].rearrange("p t (n i) -> p n t i", i=4),
+                )
+            for n0, n1 in parts:
+                nc.vector.quantize_mx(
+                    out=y_q[:, CHUNK * c + n0 : CHUNK * c + n1].bitcast(FP8X4),
+                    scales=y_s[:, CHUNK * c + n0 : CHUNK * c + n1],
+                    in_=y_bf[c][:, n0:n1, :].rearrange("p n t -> p (n t)"),
+                )
             nc.sync.dma_start(out_words[:, cols(c)], y_q[:, cols(c)].bitcast(I32))
         for q in range(4):
-            nc.sync.dma_start(out_2[0, 4 * q : 4 * q + 4, :].bitcast(I32), y_s[32 * q : 32 * q + 4, :].bitcast(I32))
+            queue = nc.sync if q < 2 else nc.scalar
+            queue.dma_start(out_2[0, 4 * q : 4 * q + 4, :].bitcast(I32), y_s[32 * q : 32 * q + 4, :].bitcast(I32))

@@ -21,7 +21,6 @@ K_PASS = P * PACK
 PASSES = K // K_PASS
 CHUNK = 128
 CHUNKS = S // CHUNK
-HALF = H // 2
 
 
 def tile_picked_zskip_relu_po_kernel(
@@ -49,7 +48,7 @@ def tile_picked_zskip_relu_po_kernel(
         w2_d = tile([P, 2 * N], U8, "w2_d")
         w3s_d = tile([P, PASSES, N], U8, "w3s_d")
         w2s_d = tile([P, N], U8, "w2s_d")
-        w1_raw = [[tile([P, PACK, HALF], F32, f"w1_raw{o}{u}") for u in range(2)] for o in range(PASSES)]
+        w1_raw = [tile([P, PACK, H], F32, f"w1_raw{o}") for o in range(PASSES)]
         w1_bf = [tile([P, PACK, P, PACK], BF16, f"w1_bf{o}") for o in range(PASSES)]
         w1_q = [tile([P, H], U32, f"w1_q{o}") for o in range(PASSES)]
         w1_s = [tile([P, H], U8, f"w1_s{o}") for o in range(PASSES)]
@@ -70,62 +69,68 @@ def tile_picked_zskip_relu_po_kernel(
         nc.vector.memset(w3s_raw[:].rearrange("p o n -> p (o n)").bitcast(I32), 0)
         nc.vector.memset(w2s_raw[:].bitcast(I32), 0)
         nc.vector.memset(xs1[:].bitcast(I32), 0)
-        nc.scalar.activation(zero_bias[:], zero[:], ACT.Relu)
 
         def load_x(o):
             nc.sync.dma_start(xw[o][:], x_words[o].rearrange("p n t -> p (n t)").bitcast(I32))
 
-        def load_w1(o, u):
-            rows = w1[K_PASS * o : K_PASS * (o + 1), HALF * u : HALF * (u + 1)]
-            nc.sync.dma_start(w1_raw[o][u][:], rows.rearrange("(p j) c -> p j c", j=PACK))
+        def load_w1(o):
+            rows = w1[K_PASS * o : K_PASS * (o + 1), :]
+            nc.sync.dma_start(w1_raw[o][:], rows.rearrange("(p j) c -> p j c", j=PACK))
 
-        nc.sync.dma_start(offsets[:], offs)
-        nc.sync.dma_start(w2_raw[:].bitcast(I32), w2_words[0].bitcast(I32))
-        nc.sync.dma_start(w3_raw[:].bitcast(I32), w3_words.rearrange("o p n -> p o n").bitcast(I32))
-        for q in range(4):
-            nc.sync.dma_start(xs[32 * q : 32 * q + 8, :].bitcast(I32), x_scales[:, 4 * q : 4 * q + 4, :].bitcast(I32))
-        load_x(0)
-        load_w1(0, 0)
-        load_w1(1, 0)
-        for r in range(4):
+        def load_w3_scales(r):
             nc.sync.dma_start(
                 w3s_raw[r:P:32, :, :].bitcast(I32), w3_scales[:, r:16:4, :].rearrange("o q n -> q o n").bitcast(I32)
             )
-        load_w1(0, 1)
-        load_w1(1, 1)
-        for r in range(4):
-            if r == 3:
-                load_x(1)
+
+        def load_w2_scales(r):
             nc.sync.dma_start(w2s_raw[r:P:32, :].bitcast(I32), w2_scales[0, r:16:4, :].bitcast(I32))
+
+        nc.scalar.activation(zero_bias[:], zero[:], ACT.Relu)
+        nc.sync.dma_start(offsets[:], offs)
+        nc.sync.dma_start(w2_raw[:].bitcast(I32), w2_words[0].bitcast(I32))
+        for q in range(4):
+            nc.sync.dma_start(xs[32 * q : 32 * q + 8, :].bitcast(I32), x_scales[:, 4 * q : 4 * q + 4, :].bitcast(I32))
+        nc.sync.dma_start(w3_raw[:].bitcast(I32), w3_words.rearrange("o p n -> p o n").bitcast(I32))
+        load_x(0)
+        for r in range(4):
+            load_w3_scales(r)
+        load_w1(0)
+        load_w1(1)
+        for r in range(3):
+            load_w2_scales(r)
+        load_x(1)
+        load_w2_scales(3)
 
         nc.vector.tensor_copy(
             w2_d[:].rearrange("p (t m b) -> p t m b", t=PACK, b=2),
             w2_raw[:].rearrange("p (m t b) -> p t m b", t=PACK, b=2),
         )
+        nc.vector.tensor_copy(xsg[:], xs[:].indirect(offsets[:]))
+        for q in range(4):
+            nc.sync.dma_start(xs1[32 * q : 32 * q + 4, :].bitcast(I32), xsg[32 * q + 4 : 32 * q + 8, :].bitcast(I32))
         nc.vector.tensor_copy(
             w3_d[:].rearrange("p o (t m b) -> p o t m b", t=PACK, b=2),
             w3_raw[:].rearrange("p o (m t b) -> p o t m b", t=PACK, b=2),
         )
-        nc.vector.tensor_copy(xsg[:], xs[:].indirect(offsets[:]))
-        for q in range(4):
-            nc.sync.dma_start(xs1[32 * q : 32 * q + 4, :].bitcast(I32), xsg[32 * q + 4 : 32 * q + 8, :].bitcast(I32))
         nc.vector.tensor_copy(xg[0][:], xw[0][:].bitcast(U32).indirect(offsets[:]))
         nc.vector.tensor_copy(
             w3s_d[:].rearrange("p o (t m) -> p o t m", t=PACK),
             w3s_raw[:].rearrange("p o (m t) -> p o t m", t=PACK),
         )
 
-        def cast_w1(o, u, m0, m1, on_vector):
-            dst = w1_bf[o][:, :, 64 * u + m0 : 64 * u + m1, :].rearrange("p t m j -> p m t j")
-            src = w1_raw[o][u][:, :, PACK * m0 : PACK * m1].rearrange("p j (m t) -> p m t j", t=PACK)
+        def cast_w1(o, t0, t1, m0, m1, on_vector):
+            dst = w1_bf[o][:, t0:t1, m0:m1, :].rearrange("p t m j -> p m t j")
+            src = w1_raw[o][:].rearrange("p j (m t) -> p m t j", t=PACK)[:, m0:m1, t0:t1, :]
             if on_vector:
                 nc.vector.tensor_copy(dst, src)
             else:
                 nc.scalar.activation(dst, src, ACT.Copy)
 
-        def quant_w1(o):
+        def quant_w1(o, t0, t1):
             nc.vector.quantize_mx(
-                out=w1_q[o][:].bitcast(FP8X4), scales=w1_s[o][:], in_=w1_bf[o][:].rearrange("p t m j -> p (t m j)")
+                out=w1_q[o][:, P * t0 : P * t1].bitcast(FP8X4),
+                scales=w1_s[o][:, P * t0 : P * t1],
+                in_=w1_bf[o][:, t0:t1, :, :].rearrange("p t m j -> p (t m j)"),
             )
 
         def cols(i):
@@ -170,15 +175,16 @@ def tile_picked_zskip_relu_po_kernel(
 
         for c in range(CHUNKS):
             mm3(0, c)
-        cast_w1(0, 0, 0, 64, False)
-        cast_w1(1, 0, 0, 64, False)
-        cast_w1(0, 1, 0, 64, True)
-        quant_w1(0)
+        cast_w1(0, 0, 4, 0, 52, False)
+        cast_w1(0, 0, 4, 52, 128, True)
+        quant_w1(0, 0, 4)
         for c in range(CHUNKS):
             mm1(0, c)
-        cast_w1(1, 1, 0, 40, False)
-        cast_w1(1, 1, 40, 64, True)
-        quant_w1(1)
+        cast_w1(1, 2, 4, 0, 96, False)
+        cast_w1(1, 0, 2, 0, 128, True)
+        cast_w1(1, 2, 4, 96, 128, True)
+        quant_w1(1, 0, 2)
+        quant_w1(1, 2, 4)
 
         for c in range(CHUNKS):
             nc.vector.tensor_copy(xg[1][:, cols(c)], xw[1][:].bitcast(U32).indirect(offsets[:, 8 * c : 8 * (c + 1)]))

@@ -223,7 +223,9 @@ def tile_picked_zskip_relu_po_kernel(
                     scales=y_s[:, CHUNK * c + n0 : CHUNK * c + n1],
                     in_=y_bf[c][:, n0:n1, :].rearrange("p n t -> p (n t)"),
                 )
-            nc.sync.dma_start(out_words[:, cols(c)], y_q[:, cols(c)].bitcast(I32))
+            if c % 2 == 1:
+                pair = slice(CHUNK * (c - 1), CHUNK * (c + 1))
+                nc.sync.dma_start(out_words[:, pair], y_q[:, pair].bitcast(I32))
         for q in range(4):
             queue = nc.sync if q < 2 else nc.scalar
             queue.dma_start(out_2[0, 4 * q : 4 * q + 4, :].bitcast(I32), y_s[32 * q : 32 * q + 4, :].bitcast(I32))

@@ -205,8 +205,10 @@ def tile_picked_zskip_relu_po_kernel(
 
         out_rows = out_0.rearrange("(p t) n -> p t n", t=PACK)
         out_words = out_1[0].rearrange("p n t -> p (n t)").bitcast(I32)
+        mm3(1, 0)
         for c in range(CHUNKS):
-            mm3(1, c)
+            if c + 1 < CHUNKS:
+                mm3(1, c + 1)
             mm2(c)
             parts = [(0, CHUNK // 2), (CHUNK // 2, CHUNK)] if c == CHUNKS - 1 else [(0, CHUNK)]
             for n0, n1 in parts:

@@ -86,20 +86,21 @@ def tile_picked_zskip_relu_po_kernel(
             nc.sync.dma_start(w2s_raw[r:P:32, :].bitcast(I32), w2_scales[0, r:16:4, :].bitcast(I32))
 
         nc.scalar.activation(zero_bias[:], zero[:], ACT.Relu)
-        nc.sync.dma_start(offsets[:], offs)
         nc.sync.dma_start(w2_raw[:].bitcast(I32), w2_words[0].bitcast(I32))
-        for q in range(4):
-            nc.sync.dma_start(xs[32 * q : 32 * q + 8, :].bitcast(I32), x_scales[:, 4 * q : 4 * q + 4, :].bitcast(I32))
+        nc.sync.dma_start(offsets[:], offs)
+        for r in range(4):
+            nc.sync.dma_start(
+                xs[r:P:16, :].bitcast(I32), x_scales[:, r:16:4, :].rearrange("o q n -> q o n").bitcast(I32)
+            )
         nc.sync.dma_start(w3_raw[:].bitcast(I32), w3_words.rearrange("o p n -> p o n").bitcast(I32))
         load_x(0)
         for r in range(4):
             load_w3_scales(r)
         load_w1(0)
-        load_w1(1)
-        for r in range(3):
+        for r in range(4):
             load_w2_scales(r)
+        load_w1(1)
         load_x(1)
-        load_w2_scales(3)
 
         nc.vector.tensor_copy(
             w2_d[:].rearrange("p (t m b) -> p t m b", t=PACK, b=2),
@@ -107,7 +108,7 @@ def tile_picked_zskip_relu_po_kernel(
         )
         nc.vector.tensor_copy(xsg[:], xs[:].indirect(offsets[:]))
         for q in range(4):
-            nc.sync.dma_start(xs1[32 * q : 32 * q + 4, :].bitcast(I32), xsg[32 * q + 4 : 32 * q + 8, :].bitcast(I32))
+            nc.sync.dma_start(xs1[32 * q : 32 * q + 4, :].bitcast(I32), xsg[32 * q + 16 : 32 * q + 20, :].bitcast(I32))
         nc.vector.tensor_copy(
             w3_d[:].rearrange("p o (t m b) -> p o t m b", t=PACK, b=2),
             w3_raw[:].rearrange("p o (m t b) -> p o t m b", t=PACK, b=2),
@@ -143,7 +144,7 @@ def tile_picked_zskip_relu_po_kernel(
                     lhsT=w1_q[o][:, cols(t)].bitcast(FP8X4),
                     lhsT_scale=w1_s[o][:, cols(t)],
                     rhs=xg[o][:, cols(c)].bitcast(FP8X4),
-                    rhs_scale=xsg[4 * o : P, cols(c)],
+                    rhs_scale=(xsg if o == 0 else xs1)[:, cols(c)],
                     start=(o == 0 and t == 0),
                     stop=(o == PASSES - 1 and t == PACK - 1),
                 )
@@ -180,6 +181,10 @@ def tile_picked_zskip_relu_po_kernel(
         quant_w1(0, 0, 4)
         for c in range(CHUNKS):
             mm1(0, c)
+        nc.vector.tensor_copy(
+            w2s_d[:].rearrange("p (t m) -> p t m", t=PACK),
+            w2s_raw[:].rearrange("p (m t) -> p t m", t=PACK),
+        )
         cast_w1(1, 2, 4, 0, 96, False)
         cast_w1(1, 0, 2, 0, 128, True)
         cast_w1(1, 2, 4, 96, 128, True)
@@ -188,10 +193,6 @@ def tile_picked_zskip_relu_po_kernel(
 
         for c in range(CHUNKS):
             nc.vector.tensor_copy(xg[1][:, cols(c)], xw[1][:].bitcast(U32).indirect(offsets[:, 8 * c : 8 * (c + 1)]))
-        nc.vector.tensor_copy(
-            w2s_d[:].rearrange("p (t m) -> p t m", t=PACK),
-            w2s_raw[:].rearrange("p (m t) -> p t m", t=PACK),
-        )
         for c in range(CHUNKS):
             mm1(1, c)
             src = h_ps[c][:].rearrange("p t n -> p n t")

@@ -31,8 +31,8 @@ def tile_picked_zskip_relu_po_kernel(
         sb = ctx.enter_context(tc.tile_pool(name="sb", bufs=1))
         ps = ctx.enter_context(tc.psum_pool(name="ps", bufs=1))
 
-        def tile(shape, dtype, name):
-            return sb.tile(shape, dtype, name=name, align_bytes=64)
+        def tile(shape, dtype, name, tag=None):
+            return sb.tile(shape, dtype, name=name, tag=tag or name, align_bytes=64)
 
         offsets = sb.tile([P, S // 16], U16, name="offsets")
         xw = [tile([P, T], I32, f"xw{o}") for o in range(PASSES)]
@@ -42,7 +42,7 @@ def tile_picked_zskip_relu_po_kernel(
         xs1 = tile([P, S], U8, "xs1")
         w3_raw = tile([P, PASSES, 2 * N], U8, "w3_raw")
         w2_raw = tile([P, 2 * N], U8, "w2_raw")
-        w3s_raw = tile([P, PASSES, N], U8, "w3s_raw")
+        w3s_raw = tile([P, PASSES, N], U8, "w3s_raw", "w3s_raw_then_w1_q0")
         w2s_raw = tile([P, N], U8, "w2s_raw")
         w3_d = tile([P, PASSES, 2 * N], U8, "w3_d")
         w2_d = tile([P, 2 * N], U8, "w2_d")
@@ -50,7 +50,7 @@ def tile_picked_zskip_relu_po_kernel(
         w2s_d = tile([P, N], U8, "w2s_d")
         w1_raw = [tile([P, PACK, H], F32, f"w1_raw{o}") for o in range(PASSES)]
         w1_bf = [tile([P, PACK, P, PACK], BF16, f"w1_bf{o}") for o in range(PASSES)]
-        w1_q = [tile([P, H], U32, f"w1_q{o}") for o in range(PASSES)]
+        w1_q = [tile([P, H], U32, "w1_q0", "w3s_raw_then_w1_q0"), tile([P, H], U32, "w1_q1")]
         w1_s = [tile([P, H], U8, f"w1_s{o}") for o in range(PASSES)]
         h_bf = [tile([P, CHUNK, PACK], BF16, f"h_bf{c}") for c in range(CHUNKS)]
         h_q = [tile([P, CHUNK], U32, f"h_q{c}") for c in range(CHUNKS)]
@@ -86,38 +86,51 @@ def tile_picked_zskip_relu_po_kernel(
             nc.sync.dma_start(w2s_raw[r:P:32, :].bitcast(I32), w2_scales[0, r:16:4, :].bitcast(I32))
 
         nc.scalar.activation(zero_bias[:], zero[:], ACT.Relu)
-        nc.sync.dma_start(w2_raw[:].bitcast(I32), w2_words[0].bitcast(I32))
         nc.sync.dma_start(offsets[:], offs)
+        nc.sync.dma_start(w2_raw[:].bitcast(I32), w2_words[0].bitcast(I32))
+        nc.sync.dma_start(w3_raw[:].bitcast(I32), w3_words.rearrange("o p n -> p o n").bitcast(I32))
         for r in range(4):
             nc.sync.dma_start(
                 xs[r:P:16, :].bitcast(I32), x_scales[:, r:16:4, :].rearrange("o q n -> q o n").bitcast(I32)
             )
-        nc.sync.dma_start(w3_raw[:].bitcast(I32), w3_words.rearrange("o p n -> p o n").bitcast(I32))
         load_x(0)
-        for r in range(4):
-            load_w3_scales(r)
         load_w1(0)
         for r in range(4):
-            load_w2_scales(r)
+            load_w3_scales(r)
         load_w1(1)
+        for r in range(2):
+            load_w2_scales(r)
         load_x(1)
 
         nc.vector.tensor_copy(
             w2_d[:].rearrange("p (t m b) -> p t m b", t=PACK, b=2),
             w2_raw[:].rearrange("p (m t b) -> p t m b", t=PACK, b=2),
         )
-        nc.vector.tensor_copy(xsg[:], xs[:].indirect(offsets[:]))
-        for q in range(4):
-            nc.sync.dma_start(xs1[32 * q : 32 * q + 4, :].bitcast(I32), xsg[32 * q + 16 : 32 * q + 20, :].bitcast(I32))
         nc.vector.tensor_copy(
             w3_d[:].rearrange("p o (t m b) -> p o t m b", t=PACK, b=2),
             w3_raw[:].rearrange("p o (m t b) -> p o t m b", t=PACK, b=2),
         )
-        nc.vector.tensor_copy(xg[0][:], xw[0][:].bitcast(U32).indirect(offsets[:]))
-        nc.vector.tensor_copy(
-            w3s_d[:].rearrange("p o (t m) -> p o t m", t=PACK),
-            w3s_raw[:].rearrange("p o (m t) -> p o t m", t=PACK),
-        )
+        nc.vector.tensor_copy(xsg[:], xs[:].indirect(offsets[:]))
+        for q in range(4):
+            nc.sync.dma_start(xs1[32 * q : 32 * q + 4, :].bitcast(I32), xsg[32 * q + 16 : 32 * q + 20, :].bitcast(I32))
+        for r in range(2, 4):
+            load_w2_scales(r)
+
+        def gather_x(o, n0, n1):
+            nc.vector.tensor_copy(xg[o][:, n0:n1], xw[o][:].bitcast(U32).indirect(offsets[:, n0 // 16 : n1 // 16]))
+
+        gather_x(0, 0, CHUNK)
+        gather_x(0, CHUNK, S)
+        for warm in range(12):
+            nc.tensor.matmul_mx(
+                out=h_ps[CHUNKS - 1][:, warm % PACK, :],
+                lhsT=xg[0][:, 0:CHUNK].bitcast(FP8X4),
+                lhsT_scale=xsg[:, 0:CHUNK],
+                rhs=xg[0][:, 0:CHUNK].bitcast(FP8X4),
+                rhs_scale=xsg[:, 0:CHUNK],
+                start=True,
+                stop=True,
+            )
 
         def cast_w1(o, t0, t1, m0, m1, on_vector):
             dst = w1_bf[o][:, t0:t1, m0:m1, :].rearrange("p t m j -> p m t j")
@@ -174,17 +187,17 @@ def tile_picked_zskip_relu_po_kernel(
                     stop=(t == PACK - 1),
                 )
 
+        cast_w1(0, 0, 4, 0, 72, False)
+        cast_w1(0, 0, 4, 72, 128, True)
+        nc.vector.tensor_copy(
+            w3s_d[:].rearrange("p o (t m) -> p o t m", t=PACK),
+            w3s_raw[:].rearrange("p o (m t) -> p o t m", t=PACK),
+        )
         for c in range(CHUNKS):
             mm3(0, c)
-        cast_w1(0, 0, 4, 0, 52, False)
-        cast_w1(0, 0, 4, 52, 128, True)
         quant_w1(0, 0, 4)
         for c in range(CHUNKS):
             mm1(0, c)
-        nc.vector.tensor_copy(
-            w2s_d[:].rearrange("p (t m) -> p t m", t=PACK),
-            w2s_raw[:].rearrange("p (m t) -> p t m", t=PACK),
-        )
         cast_w1(1, 2, 4, 0, 96, False)
         cast_w1(1, 0, 2, 0, 128, True)
         cast_w1(1, 2, 4, 96, 128, True)
@@ -192,11 +205,17 @@ def tile_picked_zskip_relu_po_kernel(
         quant_w1(1, 2, 4)
 
         for c in range(CHUNKS):
-            nc.vector.tensor_copy(xg[1][:, cols(c)], xw[1][:].bitcast(U32).indirect(offsets[:, 8 * c : 8 * (c + 1)]))
+            gather_x(1, CHUNK * c, CHUNK * (c + 1))
+        nc.vector.tensor_copy(
+            w2s_d[:].rearrange("p (t m) -> p t m", t=PACK),
+            w2s_raw[:].rearrange("p (m t) -> p t m", t=PACK),
+        )
         for c in range(CHUNKS):
             mm1(1, c)
             src = h_ps[c][:].rearrange("p t n -> p n t")
-            if c == 1:
+            if c == 0:
+                mm3(1, 0)
+            if c == CHUNKS - 1:
                 nc.vector.tensor_scalar_max(h_bf[c][:], src, 0.0)
             else:
                 nc.scalar.activation(h_bf[c][:], src, ACT.Relu, bias=zero_bias[:])
@@ -206,7 +225,6 @@ def tile_picked_zskip_relu_po_kernel(
 
         out_rows = out_0.rearrange("(p t) n -> p t n", t=PACK)
         out_words = out_1[0].rearrange("p n t -> p (n t)").bitcast(I32)
-        mm3(1, 0)
         for c in range(CHUNKS):
             if c + 1 < CHUNKS:
                 mm3(1, c + 1)

@@ -86,9 +86,9 @@ def tile_picked_zskip_relu_po_kernel(
             nc.sync.dma_start(w2s_raw[r:P:32, :].bitcast(I32), w2_scales[0, r:16:4, :].bitcast(I32))
 
         nc.scalar.activation(zero_bias[:], zero[:], ACT.Relu)
-        nc.sync.dma_start(offsets[:], offs)
         nc.sync.dma_start(w2_raw[:].bitcast(I32), w2_words[0].bitcast(I32))
         nc.sync.dma_start(w3_raw[:].bitcast(I32), w3_words.rearrange("o p n -> p o n").bitcast(I32))
+        nc.sync.dma_start(offsets[:], offs)
         for r in range(4):
             nc.sync.dma_start(
                 xs[r:P:16, :].bitcast(I32), x_scales[:, r:16:4, :].rearrange("o q n -> q o n").bitcast(I32)
@@ -215,7 +215,7 @@ def tile_picked_zskip_relu_po_kernel(
             src = h_ps[c][:].rearrange("p t n -> p n t")
             if c == 0:
                 mm3(1, 0)
-            if c == CHUNKS - 1:
+            if c == 2:
                 nc.vector.tensor_scalar_max(h_bf[c][:], src, 0.0)
             else:
                 nc.scalar.activation(h_bf[c][:], src, ACT.Relu, bias=zero_bias[:])

@@ -133,8 +133,8 @@ def tile_picked_zskip_relu_po_kernel(
             )
 
         def cast_w1(o, t0, t1, m0, m1, on_vector):
-            dst = w1_bf[o][:, t0:t1, m0:m1, :].rearrange("p t m j -> p m t j")
-            src = w1_raw[o][:].rearrange("p j (m t) -> p m t j", t=PACK)[:, m0:m1, t0:t1, :]
+            dst = w1_bf[o][:, t0:t1, m0:m1, :].rearrange("p t m j -> p m j t")
+            src = w1_raw[o][:].rearrange("p j (m t) -> p m j t", t=PACK)[:, m0:m1, :, t0:t1]
             if on_vector:
                 nc.vector.tensor_copy(dst, src)
             else:
@@ -187,8 +187,8 @@ def tile_picked_zskip_relu_po_kernel(
                     stop=(t == PACK - 1),
                 )
 
-        cast_w1(0, 0, 4, 0, 72, False)
-        cast_w1(0, 0, 4, 72, 128, True)
+        cast_w1(0, 0, 4, 0, 64, False)
+        cast_w1(0, 0, 4, 64, 128, True)
         nc.vector.tensor_copy(
             w3s_d[:].rearrange("p o (t m) -> p o t m", t=PACK),
             w3s_raw[:].rearrange("p o (m t) -> p o t m", t=PACK),

@@ -111,8 +111,7 @@ def tile_picked_zskip_relu_po_kernel(
             w3_raw[:].rearrange("p o (m t b) -> p o t m b", t=PACK, b=2),
         )
         nc.vector.tensor_copy(xsg[:], xs[:].indirect(offsets[:]))
-        for q in range(4):
-            nc.sync.dma_start(xs1[32 * q : 32 * q + 4, :].bitcast(I32), xsg[32 * q + 16 : 32 * q + 20, :].bitcast(I32))
+        nc.sync.dma_start(xs1[0 : P - 16, :].bitcast(I32), xsg[16:P, :].bitcast(I32))
         for r in range(2, 4):
             load_w2_scales(r)
 
@@ -162,7 +161,7 @@ def tile_picked_zskip_relu_po_kernel(
                     stop=(o == PASSES - 1 and t == PACK - 1),
                 )
 
-        def mm3(o, c):
+        def mm3(o, c, last=False):
             x_scale = xsg if o == 0 else xs1
             for t in range(PACK):
                 nc.tensor.matmul_mx(
@@ -172,10 +171,10 @@ def tile_picked_zskip_relu_po_kernel(
                     rhs=xg[o][:, cols(c)].bitcast(FP8X4),
                     rhs_scale=x_scale[:, cols(c)],
                     start=(o == 0 and t == 0),
-                    stop=False,
+                    stop=(last and t == PACK - 1),
                 )
 
-        def mm2(c):
+        def mm2(c, last):
             for t in range(PACK):
                 nc.tensor.matmul_mx(
                     out=y_ps[c][:, t, :],
@@ -184,7 +183,7 @@ def tile_picked_zskip_relu_po_kernel(
                     rhs=h_q[c][:].bitcast(FP8X4),
                     rhs_scale=h_s[c][:],
                     start=False,
-                    stop=(t == PACK - 1),
+                    stop=(last and t == PACK - 1),
                 )
 
         cast_w1(0, 0, 4, 0, 64, False)
@@ -226,18 +225,23 @@ def tile_picked_zskip_relu_po_kernel(
         out_rows = out_0.rearrange("(p t) n -> p t n", t=PACK)
         out_words = out_1[0].rearrange("p n t -> p (n t)").bitcast(I32)
         for c in range(CHUNKS):
-            if c + 1 < CHUNKS:
+            if c + 2 < CHUNKS:
                 mm3(1, c + 1)
-            mm2(c)
+            mm2(c, c + 1 < CHUNKS)
+            if c + 1 == CHUNKS:
+                mm3(1, c, True)
             parts = [(0, CHUNK // 2), (CHUNK // 2, CHUNK)] if c == CHUNKS - 1 else [(0, CHUNK)]
             for n0, n1 in parts:
                 nc.scalar.copy(y[c][:, :, n0:n1], y_ps[c][:, :, n0:n1])
             nc.sync.dma_start(out_rows[:, :, cols(c)], y[c][:])
             for n0, n1 in parts:
-                nc.vector.tensor_copy(
-                    y_bf[c][:, n0:n1, :].rearrange("p (n i) t -> p n t i", i=4),
-                    y[c][:, :, n0:n1].rearrange("p t (n i) -> p n t i", i=4),
-                )
+                if n0 == 0:
+                    nc.vector.tensor_copy(
+                        y_bf[c][:, n0:n1, :].rearrange("p (n i) t -> p n t i", i=4),
+                        y[c][:, :, n0:n1].rearrange("p t (n i) -> p n t i", i=4),
+                    )
+                else:
+                    nc.scalar.copy(y_bf[c][:, n0:n1, :], y_ps[c][:, :, n0:n1].rearrange("p t n -> p n t"))
             for n0, n1 in parts:
                 nc.vector.quantize_mx(
                     out=y_q[:, CHUNK * c + n0 : CHUNK * c + n1].bitcast(FP8X4),

@@ -43,7 +43,6 @@ def tile_picked_zskip_relu_po_kernel(
         w3_raw = tile([P, PASSES, 2 * N], U8, "w3_raw")
         w2_raw = tile([P, 2 * N], U8, "w2_raw")
         w3s_raw = tile([P, PASSES, N], U8, "w3s_raw", "w3s_raw_then_w1_q0")
-        w2s_raw = tile([P, N], U8, "w2s_raw")
         w3_d = tile([P, PASSES, 2 * N], U8, "w3_d")
         w2_d = tile([P, 2 * N], U8, "w2_d")
         w3s_d = tile([P, PASSES, N], U8, "w3s_d")
@@ -64,10 +63,10 @@ def tile_picked_zskip_relu_po_kernel(
         h_ps = [ps.tile([P, PACK, CHUNK], F32, name=f"h_ps{c}") for c in range(CHUNKS)]
         y_ps = [ps.tile([P, PACK, CHUNK], F32, name=f"y_ps{c}") for c in range(CHUNKS)]
 
-        nc.vector.memset(xs[:].bitcast(I32), 0)
+        nc.gpsimd.memset(xs[:].bitcast(I32), 0)
         nc.vector.memset(zero[:], 0.0)
         nc.vector.memset(w3s_raw[:].rearrange("p o n -> p (o n)").bitcast(I32), 0)
-        nc.vector.memset(w2s_raw[:].bitcast(I32), 0)
+        nc.vector.memset(w2s_d[:].bitcast(I32), 0)
         nc.vector.memset(xs1[:].bitcast(I32), 0)
 
         def load_x(o):
@@ -82,54 +81,59 @@ def tile_picked_zskip_relu_po_kernel(
                 w3s_raw[r:P:32, :, :].bitcast(I32), w3_scales[:, r:16:4, :].rearrange("o q n -> q o n").bitcast(I32)
             )
 
-        def load_w2_scales(r):
-            nc.sync.dma_start(w2s_raw[r:P:32, :].bitcast(I32), w2_scales[0, r:16:4, :].bitcast(I32))
-
         nc.scalar.activation(zero_bias[:], zero[:], ACT.Relu)
-        nc.sync.dma_start(w2_raw[:].bitcast(I32), w2_words[0].bitcast(I32))
-        nc.sync.dma_start(w3_raw[:].bitcast(I32), w3_words.rearrange("o p n -> p o n").bitcast(I32))
-        nc.sync.dma_start(offsets[:], offs)
-        for r in range(4):
-            nc.sync.dma_start(
-                xs[r:P:16, :].bitcast(I32), x_scales[:, r:16:4, :].rearrange("o q n -> q o n").bitcast(I32)
-            )
-        load_x(0)
-        load_w1(0)
-        for r in range(4):
-            load_w3_scales(r)
-        load_w1(1)
-        for r in range(2):
-            load_w2_scales(r)
-        load_x(1)
-
-        nc.vector.tensor_copy(
-            w2_d[:].rearrange("p (t m b) -> p t m b", t=PACK, b=2),
-            w2_raw[:].rearrange("p (m t b) -> p t m b", t=PACK, b=2),
-        )
-        nc.vector.tensor_copy(
-            w3_d[:].rearrange("p o (t m b) -> p o t m b", t=PACK, b=2),
-            w3_raw[:].rearrange("p o (m t b) -> p o t m b", t=PACK, b=2),
-        )
-        nc.vector.tensor_copy(xsg[:], xs[:].indirect(offsets[:]))
-        nc.sync.dma_start(xs1[0 : P - 16, :].bitcast(I32), xsg[16:P, :].bitcast(I32))
-        for r in range(2, 4):
-            load_w2_scales(r)
 
         def gather_x(o, n0, n1):
             nc.vector.tensor_copy(xg[o][:, n0:n1], xw[o][:].bitcast(U32).indirect(offsets[:, n0 // 16 : n1 // 16]))
 
-        gather_x(0, 0, CHUNK)
-        gather_x(0, CHUNK, S)
-        for warm in range(12):
-            nc.tensor.matmul_mx(
-                out=h_ps[CHUNKS - 1][:, warm % PACK, :],
-                lhsT=xg[0][:, 0:CHUNK].bitcast(FP8X4),
-                lhsT_scale=xsg[:, 0:CHUNK],
-                rhs=xg[0][:, 0:CHUNK].bitcast(FP8X4),
-                rhs_scale=xsg[:, 0:CHUNK],
-                start=True,
-                stop=True,
+        def load_w2():
+            nc.sync.dma_start(w2_raw[:].bitcast(I32), w2_words[0].bitcast(I32))
+
+        def load_w3():
+            nc.sync.dma_start(w3_raw[:].bitcast(I32), w3_words.rearrange("o p n -> p o n").bitcast(I32))
+
+        def load_x_scales():
+            nc.sync.dma_start(offsets[:], offs)
+            for r in range(4):
+                nc.sync.dma_start(
+                    xs[r:P:16, :].bitcast(I32), x_scales[:, r:16:4, :].rearrange("o q n -> q o n").bitcast(I32)
+                )
+
+        def deal_w2():
+            nc.vector.tensor_copy(
+                w2_d[:].rearrange("p (t m b) -> p t m b", t=PACK, b=2),
+                w2_raw[:].rearrange("p (m t b) -> p t m b", t=PACK, b=2),
             )
+
+        def deal_w3():
+            nc.vector.tensor_copy(
+                w3_d[:].rearrange("p o (t m b) -> p o t m b", t=PACK, b=2),
+                w3_raw[:].rearrange("p o (m t b) -> p o t m b", t=PACK, b=2),
+            )
+
+        def gather_scales():
+            nc.vector.tensor_copy(xsg[:], xs[:].indirect(offsets[:]))
+
+        def move_scales():
+            nc.sync.dma_start(xs1[0 : P - 16, :].bitcast(I32), xsg[16:P, :].bitcast(I32))
+
+        def deal_w3s():
+            nc.vector.tensor_copy(
+                w3s_d[:].rearrange("p o (t m) -> p o t m", t=PACK),
+                w3s_raw[:].rearrange("p o (m t) -> p o t m", t=PACK),
+            )
+
+        def warm(n):
+            for i in range(n):
+                nc.tensor.matmul_mx(
+                    out=h_ps[CHUNKS - 1][:, i % PACK, :],
+                    lhsT=xg[0][:, 0:CHUNK].bitcast(FP8X4),
+                    lhsT_scale=xsg[:, 0:CHUNK],
+                    rhs=xg[0][:, 0:CHUNK].bitcast(FP8X4),
+                    rhs_scale=xsg[:, 0:CHUNK],
+                    start=True,
+                    stop=True,
+                )
 
         def cast_w1(o, t0, t1, m0, m1, on_vector):
             dst = w1_bf[o][:, t0:t1, m0:m1, :].rearrange("p t m j -> p m j t")
@@ -186,12 +190,77 @@ def tile_picked_zskip_relu_po_kernel(
                     stop=(last and t == PACK - 1),
                 )
 
+        def relu_h(c, on_vector):
+            src = h_ps[c][:].rearrange("p t n -> p n t")
+            if on_vector:
+                nc.vector.tensor_scalar_max(h_bf[c][:], src, 0.0)
+            else:
+                nc.scalar.activation(h_bf[c][:], src, ACT.Relu, bias=zero_bias[:])
+
+        def quant_h(c):
+            nc.vector.quantize_mx(
+                out=h_q[c][:].bitcast(FP8X4), scales=h_s[c][:], in_=h_bf[c][:].rearrange("p n t -> p (n t)")
+            )
+
+        out_rows = out_0.rearrange("(p t) n -> p t n", t=PACK)
+        out_words = out_1[0].rearrange("p n t -> p (n t)").bitcast(I32)
+
+        def copy_y(c, n0, n1, on_vector):
+            if on_vector:
+                nc.vector.tensor_copy(y[c][:, :, n0:n1], y_ps[c][:, :, n0:n1])
+            else:
+                nc.scalar.copy(y[c][:, :, n0:n1], y_ps[c][:, :, n0:n1])
+
+        def store_y(c):
+            nc.sync.dma_start(out_rows[:, :, cols(c)], y[c][:])
+
+        def round_y(c, n0, n1):
+            nc.vector.tensor_copy(
+                y_bf[c][:, n0:n1, :].rearrange("p (n i) t -> p n t i", i=4),
+                y[c][:, :, n0:n1].rearrange("p t (n i) -> p n t i", i=4),
+            )
+
+        def round_y_psum(c, n0, n1):
+            nc.scalar.copy(y_bf[c][:, n0:n1, :], y_ps[c][:, :, n0:n1].rearrange("p t n -> p n t"))
+
+        def quant_y(c, n0, n1):
+            nc.vector.quantize_mx(
+                out=y_q[:, CHUNK * c + n0 : CHUNK * c + n1].bitcast(FP8X4),
+                scales=y_s[:, CHUNK * c + n0 : CHUNK * c + n1],
+                in_=y_bf[c][:, n0:n1, :].rearrange("p n t -> p (n t)"),
+            )
+
+        def store_words(c0, c1):
+            nc.sync.dma_start(out_words[:, CHUNK * c0 : CHUNK * c1], y_q[:, CHUNK * c0 : CHUNK * c1].bitcast(I32))
+
+        def store_scales():
+            for q in range(4):
+                queue = nc.sync if q < 2 else nc.scalar
+                queue.dma_start(out_2[0, 4 * q : 4 * q + 4, :].bitcast(I32), y_s[32 * q : 32 * q + 4, :].bitcast(I32))
+
+        load_w3()
+        load_x_scales()
+        load_x(0)
+        load_w1(0)
+        for r in range(4):
+            load_w3_scales(r)
+        nc.sync.dma_start(w3s_raw[16:32, 0, :].bitcast(I32), w2_scales[0].bitcast(I32))
+        load_w1(1)
+        deal_w3()
+        gather_scales()
+        move_scales()
+        load_x(1)
+        load_w2()
+        gather_x(0, 0, CHUNK)
+        gather_x(0, CHUNK, S)
+        warm(12)
         cast_w1(0, 0, 4, 0, 64, False)
         cast_w1(0, 0, 4, 64, 128, True)
-        nc.vector.tensor_copy(
-            w3s_d[:].rearrange("p o (t m) -> p o t m", t=PACK),
-            w3s_raw[:].rearrange("p o (m t) -> p o t m", t=PACK),
-        )
+        deal_w3s()
+        for q in range(4):
+            nc.sync.dma_start(
+                w2s_d[32 * q : 32 * q + 4, :].bitcast(I32), w3s_d[16 + 4 * q : 20 + 4 * q, 0, :].bitcast(I32)
+            )
         for c in range(CHUNKS):
             mm3(0, c)
         quant_w1(0, 0, 4)
@@ -202,55 +271,48 @@ def tile_picked_zskip_relu_po_kernel(
         cast_w1(1, 2, 4, 96, 128, True)
         quant_w1(1, 0, 2)
         quant_w1(1, 2, 4)
-
         for c in range(CHUNKS):
             gather_x(1, CHUNK * c, CHUNK * (c + 1))
-        nc.vector.tensor_copy(
-            w2s_d[:].rearrange("p (t m) -> p t m", t=PACK),
-            w2s_raw[:].rearrange("p (m t) -> p t m", t=PACK),
-        )
-        for c in range(CHUNKS):
-            mm1(1, c)
-            src = h_ps[c][:].rearrange("p t n -> p n t")
-            if c == 0:
-                mm3(1, 0)
-            if c == 2:
-                nc.vector.tensor_scalar_max(h_bf[c][:], src, 0.0)
-            else:
-                nc.scalar.activation(h_bf[c][:], src, ACT.Relu, bias=zero_bias[:])
-            nc.vector.quantize_mx(
-                out=h_q[c][:].bitcast(FP8X4), scales=h_s[c][:], in_=h_bf[c][:].rearrange("p n t -> p (n t)")
-            )
-
-        out_rows = out_0.rearrange("(p t) n -> p t n", t=PACK)
-        out_words = out_1[0].rearrange("p n t -> p (n t)").bitcast(I32)
-        for c in range(CHUNKS):
-            if c + 2 < CHUNKS:
-                mm3(1, c + 1)
-            mm2(c, c + 1 < CHUNKS)
-            if c + 1 == CHUNKS:
-                mm3(1, c, True)
-            parts = [(0, CHUNK // 2), (CHUNK // 2, CHUNK)] if c == CHUNKS - 1 else [(0, CHUNK)]
-            for n0, n1 in parts:
-                nc.scalar.copy(y[c][:, :, n0:n1], y_ps[c][:, :, n0:n1])
-            nc.sync.dma_start(out_rows[:, :, cols(c)], y[c][:])
-            for n0, n1 in parts:
-                if n0 == 0:
-                    nc.vector.tensor_copy(
-                        y_bf[c][:, n0:n1, :].rearrange("p (n i) t -> p n t i", i=4),
-                        y[c][:, :, n0:n1].rearrange("p t (n i) -> p n t i", i=4),
-                    )
-                else:
-                    nc.scalar.copy(y_bf[c][:, n0:n1, :], y_ps[c][:, :, n0:n1].rearrange("p t n -> p n t"))
-            for n0, n1 in parts:
-                nc.vector.quantize_mx(
-                    out=y_q[:, CHUNK * c + n0 : CHUNK * c + n1].bitcast(FP8X4),
-                    scales=y_s[:, CHUNK * c + n0 : CHUNK * c + n1],
-                    in_=y_bf[c][:, n0:n1, :].rearrange("p n t -> p (n t)"),
-                )
-            if c % 2 == 1:
-                pair = slice(CHUNK * (c - 1), CHUNK * (c + 1))
-                nc.sync.dma_start(out_words[:, pair], y_q[:, pair].bitcast(I32))
-        for q in range(4):
-            queue = nc.sync if q < 2 else nc.scalar
-            queue.dma_start(out_2[0, 4 * q : 4 * q + 4, :].bitcast(I32), y_s[32 * q : 32 * q + 4, :].bitcast(I32))
+        deal_w2()
+        mm1(1, 0)
+        mm3(1, 0)
+        relu_h(0, False)
+        quant_h(0)
+        mm1(1, 1)
+        relu_h(1, False)
+        quant_h(1)
+        mm1(1, 2)
+        relu_h(2, True)
+        quant_h(2)
+        mm1(1, 3)
+        relu_h(3, False)
+        quant_h(3)
+        mm3(1, 1)
+        mm2(0, True)
+        copy_y(0, 0, 128, False)
+        store_y(0)
+        round_y(0, 0, 128)
+        quant_y(0, 0, 128)
+        mm2(1, True)
+        copy_y(1, 0, 128, False)
+        store_y(1)
+        round_y(1, 0, 128)
+        quant_y(1, 0, 128)
+        store_words(0, 2)
+        mm2(2, False)
+        mm3(1, 2, True)
+        copy_y(2, 0, 128, False)
+        store_y(2)
+        round_y(2, 0, 128)
+        quant_y(2, 0, 128)
+        mm2(3, False)
+        mm3(1, 3, True)
+        copy_y(3, 0, 64, False)
+        copy_y(3, 64, 128, False)
+        store_y(3)
+        round_y(3, 0, 64)
+        round_y_psum(3, 64, 128)
+        quant_y(3, 0, 64)
+        quant_y(3, 64, 128)
+        store_words(2, 4)
+        store_scales()

@@ -36,8 +36,10 @@ def tile_picked_zskip_relu_po_kernel(
 
         offsets = sb.tile([P, S // 16], U16, name="offsets")
         xw = [tile([P, T], I32, f"xw{o}") for o in range(PASSES)]
-        xs = tile([P, T], U8, "xs")
-        xg = [tile([P, S], U32, f"xg{o}") for o in range(PASSES)]
+        xs = tile([P, T], U8, "xs", "xs_then_xg0_rest")
+        xg0_first = tile([P, CHUNK], U32, "xg0_first")
+        xg0_rest = tile([P, S - CHUNK], U32, "xg0_rest", "xs_then_xg0_rest")
+        xg1 = tile([P, S], U32, "xg1")
         xsg = tile([P, S], U8, "xsg")
         xs1 = tile([P, S], U8, "xs1")
         w3_raw = tile([P, PASSES, 2 * N], U8, "w3_raw")
@@ -63,7 +65,7 @@ def tile_picked_zskip_relu_po_kernel(
         h_ps = [ps.tile([P, PACK, CHUNK], F32, name=f"h_ps{c}") for c in range(CHUNKS)]
         y_ps = [ps.tile([P, PACK, CHUNK], F32, name=f"y_ps{c}") for c in range(CHUNKS)]
 
-        nc.gpsimd.memset(xs[:].bitcast(I32), 0)
+        nc.vector.memset(xs[:].bitcast(I32), 0)
         nc.vector.memset(zero[:], 0.0)
         nc.vector.memset(w3s_raw[:].rearrange("p o n -> p (o n)").bitcast(I32), 0)
         nc.vector.memset(w2s_d[:].bitcast(I32), 0)
@@ -83,8 +85,13 @@ def tile_picked_zskip_relu_po_kernel(
 
         nc.scalar.activation(zero_bias[:], zero[:], ACT.Relu)
 
+        def picked(o, n0, n1):
+            if o == 1:
+                return xg1[:, n0:n1]
+            return xg0_first[:, n0:n1] if n1 <= CHUNK else xg0_rest[:, n0 - CHUNK : n1 - CHUNK]
+
         def gather_x(o, n0, n1):
-            nc.vector.tensor_copy(xg[o][:, n0:n1], xw[o][:].bitcast(U32).indirect(offsets[:, n0 // 16 : n1 // 16]))
+            nc.vector.tensor_copy(picked(o, n0, n1), xw[o][:].bitcast(U32).indirect(offsets[:, n0 // 16 : n1 // 16]))
 
         def load_w2():
             nc.sync.dma_start(w2_raw[:].bitcast(I32), w2_words[0].bitcast(I32))
@@ -114,9 +121,6 @@ def tile_picked_zskip_relu_po_kernel(
         def gather_scales():
             nc.vector.tensor_copy(xsg[:], xs[:].indirect(offsets[:]))
 
-        def move_scales():
-            nc.sync.dma_start(xs1[0 : P - 16, :].bitcast(I32), xsg[16:P, :].bitcast(I32))
-
         def deal_w3s():
             nc.vector.tensor_copy(
                 w3s_d[:].rearrange("p o (t m) -> p o t m", t=PACK),
@@ -127,9 +131,9 @@ def tile_picked_zskip_relu_po_kernel(
             for i in range(n):
                 nc.tensor.matmul_mx(
                     out=h_ps[CHUNKS - 1][:, i % PACK, :],
-                    lhsT=xg[0][:, 0:CHUNK].bitcast(FP8X4),
+                    lhsT=xg0_first[:].bitcast(FP8X4),
                     lhsT_scale=xsg[:, 0:CHUNK],
-                    rhs=xg[0][:, 0:CHUNK].bitcast(FP8X4),
+                    rhs=xg0_first[:].bitcast(FP8X4),
                     rhs_scale=xsg[:, 0:CHUNK],
                     start=True,
                     stop=True,
@@ -159,7 +163,7 @@ def tile_picked_zskip_relu_po_kernel(
                     out=h_ps[c][:, t, :],
                     lhsT=w1_q[o][:, cols(t)].bitcast(FP8X4),
                     lhsT_scale=w1_s[o][:, cols(t)],
-                    rhs=xg[o][:, cols(c)].bitcast(FP8X4),
+                    rhs=picked(o, CHUNK * c, CHUNK * (c + 1)).bitcast(FP8X4),
                     rhs_scale=(xsg if o == 0 else xs1)[:, cols(c)],
                     start=(o == 0 and t == 0),
                     stop=(o == PASSES - 1 and t == PACK - 1),
@@ -172,7 +176,7 @@ def tile_picked_zskip_relu_po_kernel(
                     out=y_ps[c][:, t, :],
                     lhsT=w3_d[:, o, 256 * t : 256 * (t + 1)].bitcast(FP4X4),
                     lhsT_scale=w3s_d[:, o, cols(t)],
-                    rhs=xg[o][:, cols(c)].bitcast(FP8X4),
+                    rhs=picked(o, CHUNK * c, CHUNK * (c + 1)).bitcast(FP8X4),
                     rhs_scale=x_scale[:, cols(c)],
                     start=(o == 0 and t == 0),
                     stop=(last and t == PACK - 1),
@@ -239,8 +243,8 @@ def tile_picked_zskip_relu_po_kernel(
                 queue.dma_start(out_2[0, 4 * q : 4 * q + 4, :].bitcast(I32), y_s[32 * q : 32 * q + 4, :].bitcast(I32))
 
         load_w3()
-        load_x_scales()
         load_x(0)
+        load_x_scales()
         load_w1(0)
         for r in range(4):
             load_w3_scales(r)
@@ -248,14 +252,15 @@ def tile_picked_zskip_relu_po_kernel(
         load_w1(1)
         deal_w3()
         gather_scales()
-        move_scales()
+        nc.sync.dma_start(xs1[0:4, :].bitcast(I32), xsg[16:20, :].bitcast(I32))
         load_x(1)
         load_w2()
+        nc.sync.dma_start(xs1[32 : P - 16, :].bitcast(I32), xsg[48:P, :].bitcast(I32))
         gather_x(0, 0, CHUNK)
         gather_x(0, CHUNK, S)
         warm(12)
-        cast_w1(0, 0, 4, 0, 64, False)
-        cast_w1(0, 0, 4, 64, 128, True)
+        cast_w1(0, 0, 4, 0, 72, False)
+        cast_w1(0, 0, 4, 72, 128, True)
         deal_w3s()
         for q in range(4):
             nc.sync.dma_start(
@@ -293,14 +298,13 @@ def tile_picked_zskip_relu_po_kernel(
         store_y(0)
         round_y(0, 0, 128)
         quant_y(0, 0, 128)
+        mm3(1, 2)
         mm2(1, True)
         copy_y(1, 0, 128, False)
         store_y(1)
         round_y(1, 0, 128)
         quant_y(1, 0, 128)
-        store_words(0, 2)
-        mm2(2, False)
-        mm3(1, 2, True)
+        mm2(2, True)
         copy_y(2, 0, 128, False)
         store_y(2)
         round_y(2, 0, 128)
@@ -314,5 +318,5 @@ def tile_picked_zskip_relu_po_kernel(
         round_y_psum(3, 64, 128)
         quant_y(3, 0, 64)
         quant_y(3, 64, 128)
-        store_words(2, 4)
+        store_words(0, 4)
         store_scales()

@@ -107,9 +107,9 @@ def tile_picked_zskip_relu_po_kernel(
                 )
 
         def deal_w2():
-            nc.vector.tensor_copy(
-                w2_d[:].rearrange("p (t m b) -> p t m b", t=PACK, b=2),
-                w2_raw[:].rearrange("p (m t b) -> p t m b", t=PACK, b=2),
+            nc.gpsimd.tensor_copy(
+                w2_d[:].rearrange("p (t m b) -> p t b m", t=PACK, b=2),
+                w2_raw[:].rearrange("p (m t b) -> p t b m", t=PACK, b=2),
             )
 
         def deal_w3():

@@ -46,11 +46,11 @@ def tile_picked_zskip_relu_po_kernel(
         w2_raw = tile([P, 2 * N], U8, "w2_raw")
         w3s_raw = tile([P, PASSES, N], U8, "w3s_raw", "w3s_raw_then_w1_q0")
         w3_d = tile([P, PASSES, 2 * N], U8, "w3_d")
-        w2_d = tile([P, 2 * N], U8, "w2_d")
         w3s_d = tile([P, PASSES, N], U8, "w3s_d")
         w2s_d = tile([P, N], U8, "w2s_d")
         w1_raw = [tile([P, PACK, H], F32, f"w1_raw{o}") for o in range(PASSES)]
         w1_bf = [tile([P, PACK, P, PACK], BF16, f"w1_bf{o}") for o in range(PASSES)]
+        w2_d = tile([P, 2 * N], U8, "w2_d", "w1_bf1")
         w1_q = [tile([P, H], U32, "w1_q0", "w3s_raw_then_w1_q0"), tile([P, H], U32, "w1_q1")]
         w1_s = [tile([P, H], U8, f"w1_s{o}") for o in range(PASSES)]
         h_bf = [tile([P, CHUNK, PACK], BF16, f"h_bf{c}") for c in range(CHUNKS)]
@@ -120,6 +120,9 @@ def tile_picked_zskip_relu_po_kernel(
 
         def gather_scales():
             nc.vector.tensor_copy(xsg[:], xs[:].indirect(offsets[:]))
+
+        def move_scales():
+            nc.sync.dma_start(xs1[0 : P - 16, :].bitcast(I32), xsg[16:P, :].bitcast(I32))
 
         def deal_w3s():
             nc.vector.tensor_copy(
@@ -252,15 +255,14 @@ def tile_picked_zskip_relu_po_kernel(
         load_w1(1)
         deal_w3()
         gather_scales()
-        nc.sync.dma_start(xs1[0:4, :].bitcast(I32), xsg[16:20, :].bitcast(I32))
         load_x(1)
+        move_scales()
         load_w2()
-        nc.sync.dma_start(xs1[32 : P - 16, :].bitcast(I32), xsg[48:P, :].bitcast(I32))
         gather_x(0, 0, CHUNK)
         gather_x(0, CHUNK, S)
         warm(12)
-        cast_w1(0, 0, 4, 0, 72, False)
-        cast_w1(0, 0, 4, 72, 128, True)
+        cast_w1(0, 0, 4, 0, 80, False)
+        cast_w1(0, 0, 4, 80, 128, True)
         deal_w3s()
         for q in range(4):
             nc.sync.dma_start(
@@ -271,23 +273,23 @@ def tile_picked_zskip_relu_po_kernel(
         quant_w1(0, 0, 4)
         for c in range(CHUNKS):
             mm1(0, c)
-        cast_w1(1, 2, 4, 0, 96, False)
+        cast_w1(1, 2, 4, 0, 128, False)
         cast_w1(1, 0, 2, 0, 128, True)
-        cast_w1(1, 2, 4, 96, 128, True)
         quant_w1(1, 0, 2)
+        gather_x(1, 0, CHUNK)
         quant_w1(1, 2, 4)
-        for c in range(CHUNKS):
+        for c in range(1, CHUNKS):
             gather_x(1, CHUNK * c, CHUNK * (c + 1))
         deal_w2()
-        mm1(1, 0)
         mm3(1, 0)
-        relu_h(0, False)
+        mm1(1, 0)
+        relu_h(0, True)
         quant_h(0)
         mm1(1, 1)
         relu_h(1, False)
         quant_h(1)
         mm1(1, 2)
-        relu_h(2, True)
+        relu_h(2, False)
         quant_h(2)
         mm1(1, 3)
         relu_h(3, False)

@@ -29,6 +29,7 @@ def tile_picked_zskip_relu_po_kernel(
     nc = tc.nc
     with ExitStack() as ctx:
         sb = ctx.enter_context(tc.tile_pool(name="sb", bufs=1))
+        reused = ctx.enter_context(tc.tile_pool(name="reused", bufs=1))
         ps = ctx.enter_context(tc.psum_pool(name="ps", bufs=1))
 
         def tile(shape, dtype, name, tag=None):
@@ -44,15 +45,21 @@ def tile_picked_zskip_relu_po_kernel(
         xs1 = tile([P, S], U8, "xs1")
         w3_raw = tile([P, PASSES, 2 * N], U8, "w3_raw")
         w2_raw = tile([P, 2 * N], U8, "w2_raw")
-        w3s_raw = tile([P, PASSES, N], U8, "w3s_raw", "w3s_raw_then_w1_q0")
+        w3s_raw = reused.tile([P, PASSES, N], U8, name="w3s_raw", offset=0, align_bytes=64)
         w3_d = tile([P, PASSES, 2 * N], U8, "w3_d")
         w3s_d = tile([P, PASSES, N], U8, "w3s_d")
         w2s_d = tile([P, N], U8, "w2s_d")
         w1_raw = [tile([P, PACK, H], F32, f"w1_raw{o}") for o in range(PASSES)]
-        w1_bf = [tile([P, PACK, P, PACK], BF16, f"w1_bf{o}") for o in range(PASSES)]
-        w2_d = tile([P, 2 * N], U8, "w2_d", "w1_bf1")
-        w1_q = [tile([P, H], U32, "w1_q0", "w3s_raw_then_w1_q0"), tile([P, H], U32, "w1_q1")]
-        w1_s = [tile([P, H], U8, f"w1_s{o}") for o in range(PASSES)]
+        w1_bf = [
+            [
+                tile([P, 2, P, PACK], BF16, "w1_bf00"),
+                reused.tile([P, 2, P, PACK], BF16, name="w1_bf01", offset=N, align_bytes=64),
+            ],
+            [tile([P, 2, P, PACK], BF16, "w1_bf10"), tile([P, 2, P, PACK], BF16, "w1_bf11")],
+        ]
+        w2_d = tile([P, 2 * N], U8, "w2_d", "w1_bf11")
+        w1_q = [tile([P, H], U32, f"w1_q{o}") for o in range(PASSES)]
+        w1_s = [reused.tile([P, H], U8, name="w1_s0", offset=0, align_bytes=64), tile([P, H], U8, "w1_s1")]
         h_bf = [tile([P, CHUNK, PACK], BF16, f"h_bf{c}") for c in range(CHUNKS)]
         h_q = [tile([P, CHUNK], U32, f"h_q{c}") for c in range(CHUNKS)]
         h_s = [tile([P, CHUNK], U8, f"h_s{c}") for c in range(CHUNKS)]
@@ -143,7 +150,7 @@ def tile_picked_zskip_relu_po_kernel(
                 )
 
         def cast_w1(o, t0, t1, m0, m1, on_vector):
-            dst = w1_bf[o][:, t0:t1, m0:m1, :].rearrange("p t m j -> p m j t")
+            dst = w1_bf[o][t0 // 2][:, :, m0:m1, :].rearrange("p t m j -> p m j t")
             src = w1_raw[o][:].rearrange("p j (m t) -> p m j t", t=PACK)[:, m0:m1, :, t0:t1]
             if on_vector:
                 nc.vector.tensor_copy(dst, src)
@@ -154,7 +161,7 @@ def tile_picked_zskip_relu_po_kernel(
             nc.vector.quantize_mx(
                 out=w1_q[o][:, P * t0 : P * t1].bitcast(FP8X4),
                 scales=w1_s[o][:, P * t0 : P * t1],
-                in_=w1_bf[o][:, t0:t1, :, :].rearrange("p t m j -> p (t m j)"),
+                in_=w1_bf[o][t0 // 2][:].rearrange("p t m j -> p (t m j)"),
             )
 
         def cols(i):
@@ -261,16 +268,18 @@ def tile_picked_zskip_relu_po_kernel(
         gather_x(0, 0, CHUNK)
         gather_x(0, CHUNK, S)
         warm(12)
-        cast_w1(0, 0, 4, 0, 80, False)
-        cast_w1(0, 0, 4, 80, 128, True)
         deal_w3s()
+        cast_w1(0, 0, 2, 0, 128, False)
+        cast_w1(0, 2, 4, 0, 48, False)
+        cast_w1(0, 2, 4, 48, 128, True)
         for q in range(4):
             nc.sync.dma_start(
                 w2s_d[32 * q : 32 * q + 4, :].bitcast(I32), w3s_d[16 + 4 * q : 20 + 4 * q, 0, :].bitcast(I32)
             )
         for c in range(CHUNKS):
             mm3(0, c)
-        quant_w1(0, 0, 4)
+        quant_w1(0, 0, 2)
+        quant_w1(0, 2, 4)
         for c in range(CHUNKS):
             mm1(0, c)
         cast_w1(1, 2, 4, 0, 128, False)
@@ -283,10 +292,10 @@ def tile_picked_zskip_relu_po_kernel(
         deal_w2()
         mm3(1, 0)
         mm1(1, 0)
-        relu_h(0, True)
+        relu_h(0, False)
         quant_h(0)
         mm1(1, 1)
-        relu_h(1, False)
+        relu_h(1, True)
         quant_h(1)
         mm1(1, 2)
         relu_h(2, False)
@@ -302,7 +311,7 @@ def tile_picked_zskip_relu_po_kernel(
         quant_y(0, 0, 128)
         mm3(1, 2)
         mm2(1, True)
-        copy_y(1, 0, 128, False)
+        copy_y(1, 0, 128, True)
         store_y(1)
         round_y(1, 0, 128)
         quant_y(1, 0, 128)
@@ -313,12 +322,9 @@ def tile_picked_zskip_relu_po_kernel(
         quant_y(2, 0, 128)
         mm2(3, False)
         mm3(1, 3, True)
-        copy_y(3, 0, 64, False)
-        copy_y(3, 64, 128, False)
+        copy_y(3, 0, 128, False)
         store_y(3)
-        round_y(3, 0, 64)
-        round_y_psum(3, 64, 128)
-        quant_y(3, 0, 64)
-        quant_y(3, 64, 128)
+        round_y_psum(3, 0, 128)
+        quant_y(3, 0, 128)
         store_words(0, 4)
         store_scales()

@@ -305,8 +305,9 @@ def tile_picked_zskip_relu_po_kernel(
         quant_h(3)
         mm3(1, 1)
         mm2(0, True)
-        copy_y(0, 0, 128, False)
-        store_y(0)
+        for t0 in (0, 2):
+            nc.scalar.copy(y[0][:, t0 : t0 + 2, :], y_ps[0][:, t0 : t0 + 2, :])
+            nc.sync.dma_start(out_rows[:, t0 : t0 + 2, cols(0)], y[0][:, t0 : t0 + 2, :])
         round_y(0, 0, 128)
         quant_y(0, 0, 128)
         mm3(1, 2)

@@ -33,7 +33,7 @@ def tile_picked_zskip_relu_po_kernel(
         ps = ctx.enter_context(tc.psum_pool(name="ps", bufs=1))
 
         def tile(shape, dtype, name, tag=None):
-            return sb.tile(shape, dtype, name=name, tag=tag or name, align_bytes=64)
+            return sb.tile(shape, dtype, name=name, tag=tag or name, align_bytes=256)
 
         offsets = sb.tile([P, S // 16], U16, name="offsets")
         xw = [tile([P, T], I32, f"xw{o}") for o in range(PASSES)]
@@ -45,7 +45,7 @@ def tile_picked_zskip_relu_po_kernel(
         xs1 = tile([P, S], U8, "xs1")
         w3_raw = tile([P, PASSES, 2 * N], U8, "w3_raw")
         w2_raw = tile([P, 2 * N], U8, "w2_raw")
-        w3s_raw = reused.tile([P, PASSES, N], U8, name="w3s_raw", offset=0, align_bytes=64)
+        w3s_raw = reused.tile([P, PASSES, N], U8, name="w3s_raw", offset=0, align_bytes=256)
         w3_d = tile([P, PASSES, 2 * N], U8, "w3_d")
         w3s_d = tile([P, PASSES, N], U8, "w3s_d")
         w2s_d = tile([P, N], U8, "w2s_d")
@@ -53,13 +53,13 @@ def tile_picked_zskip_relu_po_kernel(
         w1_bf = [
             [
                 tile([P, 2, P, PACK], BF16, "w1_bf00"),
-                reused.tile([P, 2, P, PACK], BF16, name="w1_bf01", offset=N, align_bytes=64),
+                reused.tile([P, 2, P, PACK], BF16, name="w1_bf01", offset=N, align_bytes=256),
             ],
             [tile([P, 2, P, PACK], BF16, "w1_bf10"), tile([P, 2, P, PACK], BF16, "w1_bf11")],
         ]
         w2_d = tile([P, 2 * N], U8, "w2_d", "w1_bf11")
         w1_q = [tile([P, H], U32, f"w1_q{o}") for o in range(PASSES)]
-        w1_s = [reused.tile([P, H], U8, name="w1_s0", offset=0, align_bytes=64), tile([P, H], U8, "w1_s1")]
+        w1_s = [reused.tile([P, H], U8, name="w1_s0", offset=0, align_bytes=256), tile([P, H], U8, "w1_s1")]
         h_bf = [tile([P, CHUNK, PACK], BF16, f"h_bf{c}") for c in range(CHUNKS)]
         h_q = [tile([P, CHUNK], U32, f"h_q{c}") for c in range(CHUNKS)]
         h_s = [tile([P, CHUNK], U8, f"h_s{c}") for c in range(CHUNKS)]

@@ -30,6 +30,7 @@ def tile_picked_zskip_relu_po_kernel(
     with ExitStack() as ctx:
         sb = ctx.enter_context(tc.tile_pool(name="sb", bufs=1))
         reused = ctx.enter_context(tc.tile_pool(name="reused", bufs=1))
+        late = ctx.enter_context(tc.tile_pool(name="late", bufs=1))
         ps = ctx.enter_context(tc.psum_pool(name="ps", bufs=1))
 
         def tile(shape, dtype, name, tag=None):
@@ -43,10 +44,9 @@ def tile_picked_zskip_relu_po_kernel(
         xg1 = tile([P, S], U32, "xg1")
         xsg = tile([P, S], U8, "xsg")
         xs1 = tile([P, S], U8, "xs1")
-        w3_raw = tile([P, PASSES, 2 * N], U8, "w3_raw")
+        w3_raw = [tile([P, 2 * N], U8, f"w3_raw{o}") for o in range(PASSES)]
         w2_raw = tile([P, 2 * N], U8, "w2_raw")
         w3s_raw = reused.tile([P, PASSES, N], U8, name="w3s_raw", offset=0, align_bytes=256)
-        w3_d = tile([P, PASSES, 2 * N], U8, "w3_d")
         w3s_d = tile([P, PASSES, N], U8, "w3s_d")
         w2s_d = tile([P, N], U8, "w2s_d")
         w1_raw = [tile([P, PACK, H], F32, f"w1_raw{o}") for o in range(PASSES)]
@@ -55,9 +55,13 @@ def tile_picked_zskip_relu_po_kernel(
                 tile([P, 2, P, PACK], BF16, "w1_bf00"),
                 reused.tile([P, 2, P, PACK], BF16, name="w1_bf01", offset=N, align_bytes=256),
             ],
-            [tile([P, 2, P, PACK], BF16, "w1_bf10"), tile([P, 2, P, PACK], BF16, "w1_bf11")],
+            [
+                tile([P, 2, P, PACK], BF16, "w1_bf10"),
+                late.tile([P, 2, P, PACK], BF16, name="w1_bf11", offset=0, align_bytes=256),
+            ],
         ]
-        w2_d = tile([P, 2 * N], U8, "w2_d", "w1_bf11")
+        w3_d = [tile([P, 2 * N], U8, "w3_d0"), late.tile([P, 2 * N], U8, name="w3_d1", offset=0, align_bytes=256)]
+        w2_d = late.tile([P, 2 * N], U8, name="w2_d", offset=2 * N, align_bytes=256)
         w1_q = [tile([P, H], U32, f"w1_q{o}") for o in range(PASSES)]
         w1_s = [reused.tile([P, H], U8, name="w1_s0", offset=0, align_bytes=256), tile([P, H], U8, "w1_s1")]
         h_bf = [tile([P, CHUNK, PACK], BF16, f"h_bf{c}") for c in range(CHUNKS)]
@@ -103,8 +107,8 @@ def tile_picked_zskip_relu_po_kernel(
         def load_w2():
             nc.sync.dma_start(w2_raw[:].bitcast(I32), w2_words[0].bitcast(I32))
 
-        def load_w3():
-            nc.sync.dma_start(w3_raw[:].bitcast(I32), w3_words.rearrange("o p n -> p o n").bitcast(I32))
+        def load_w3(o):
+            nc.sync.dma_start(w3_raw[o][:].bitcast(I32), w3_words[o].bitcast(I32))
 
         def load_x_scales():
             nc.sync.dma_start(offsets[:], offs)
@@ -113,16 +117,10 @@ def tile_picked_zskip_relu_po_kernel(
                     xs[r:P:16, :].bitcast(I32), x_scales[:, r:16:4, :].rearrange("o q n -> q o n").bitcast(I32)
                 )
 
-        def deal_w2():
-            nc.gpsimd.tensor_copy(
-                w2_d[:].rearrange("p (t m b) -> p t b m", t=PACK, b=2),
-                w2_raw[:].rearrange("p (m t b) -> p t b m", t=PACK, b=2),
-            )
-
-        def deal_w3():
-            nc.vector.tensor_copy(
-                w3_d[:].rearrange("p o (t m b) -> p o t m b", t=PACK, b=2),
-                w3_raw[:].rearrange("p o (m t b) -> p o t m b", t=PACK, b=2),
+        def deal_words(engine, dealt, raw):
+            engine.tensor_copy(
+                dealt[:].bitcast(U16).rearrange("p (t m) -> p t m", t=PACK),
+                raw[:].bitcast(U16).rearrange("p (m t) -> p t m", t=PACK),
             )
 
         def gather_scales():
@@ -140,11 +138,11 @@ def tile_picked_zskip_relu_po_kernel(
         def warm(n):
             for i in range(n):
                 nc.tensor.matmul_mx(
-                    out=h_ps[CHUNKS - 1][:, i % PACK, :],
+                    out=h_ps[CHUNKS - 1 - i % 2][:].rearrange("p t n -> p (t n)"),
                     lhsT=xg0_first[:].bitcast(FP8X4),
-                    lhsT_scale=xsg[:, 0:CHUNK],
-                    rhs=xg0_first[:].bitcast(FP8X4),
-                    rhs_scale=xsg[:, 0:CHUNK],
+                    lhsT_scale=xs1[:, 0:CHUNK],
+                    rhs=w3_d[0][:].bitcast(FP4X4),
+                    rhs_scale=xs1[:],
                     start=True,
                     stop=True,
                 )
@@ -184,7 +182,7 @@ def tile_picked_zskip_relu_po_kernel(
             for t in range(PACK):
                 nc.tensor.matmul_mx(
                     out=y_ps[c][:, t, :],
-                    lhsT=w3_d[:, o, 256 * t : 256 * (t + 1)].bitcast(FP4X4),
+                    lhsT=w3_d[o][:, 256 * t : 256 * (t + 1)].bitcast(FP4X4),
                     lhsT_scale=w3s_d[:, o, cols(t)],
                     rhs=picked(o, CHUNK * c, CHUNK * (c + 1)).bitcast(FP8X4),
                     rhs_scale=x_scale[:, cols(c)],
@@ -252,7 +250,7 @@ def tile_picked_zskip_relu_po_kernel(
                 queue = nc.sync if q < 2 else nc.scalar
                 queue.dma_start(out_2[0, 4 * q : 4 * q + 4, :].bitcast(I32), y_s[32 * q : 32 * q + 4, :].bitcast(I32))
 
-        load_w3()
+        load_w3(0)
         load_x(0)
         load_x_scales()
         load_w1(0)
@@ -260,14 +258,15 @@ def tile_picked_zskip_relu_po_kernel(
             load_w3_scales(r)
         nc.sync.dma_start(w3s_raw[16:32, 0, :].bitcast(I32), w2_scales[0].bitcast(I32))
         load_w1(1)
-        deal_w3()
+        deal_words(nc.vector, w3_d[0], w3_raw[0])
+        gather_x(0, 0, CHUNK)
+        warm(4)
         gather_scales()
         load_x(1)
         move_scales()
+        load_w3(1)
         load_w2()
-        gather_x(0, 0, CHUNK)
         gather_x(0, CHUNK, S)
-        warm(12)
         deal_w3s()
         cast_w1(0, 0, 2, 0, 128, False)
         cast_w1(0, 2, 4, 0, 48, False)
@@ -289,8 +288,8 @@ def tile_picked_zskip_relu_po_kernel(
         quant_w1(1, 2, 4)
         for c in range(1, CHUNKS):
             gather_x(1, CHUNK * c, CHUNK * (c + 1))
-        deal_w2()
-        mm3(1, 0)
+        deal_words(nc.gpsimd, w3_d[1], w3_raw[1])
+        deal_words(nc.gpsimd, w2_d, w2_raw)
         mm1(1, 0)
         relu_h(0, False)
         quant_h(0)
@@ -303,6 +302,7 @@ def tile_picked_zskip_relu_po_kernel(
         mm1(1, 3)
         relu_h(3, False)
         quant_h(3)
+        mm3(1, 0)
         mm3(1, 1)
         mm2(0, True)
         for t0 in (0, 2):

@@ -46,8 +46,9 @@ def tile_picked_zskip_relu_po_kernel(
         xs1 = tile([P, S], U8, "xs1")
         w3_raw = [tile([P, 2 * N], U8, f"w3_raw{o}") for o in range(PASSES)]
         w2_raw = tile([P, 2 * N], U8, "w2_raw")
-        w3s_raw = reused.tile([P, PASSES, N], U8, name="w3s_raw", offset=0, align_bytes=256)
-        w3s_d = tile([P, PASSES, N], U8, "w3s_d")
+        w3s_raw = reused.tile([P, N], U8, name="w3s_raw", offset=N // 2, align_bytes=256)
+        w3s_d = tile([P, N], U8, "w3s_d")
+        w3s1 = tile([P, N], U8, "w3s1")
         w2s_d = tile([P, N], U8, "w2s_d")
         w1_raw = [tile([P, PACK, H], F32, f"w1_raw{o}") for o in range(PASSES)]
         w1_bf = [
@@ -78,9 +79,10 @@ def tile_picked_zskip_relu_po_kernel(
 
         nc.vector.memset(xs[:].bitcast(I32), 0)
         nc.vector.memset(zero[:], 0.0)
-        nc.vector.memset(w3s_raw[:].rearrange("p o n -> p (o n)").bitcast(I32), 0)
+        nc.vector.memset(w3s_raw[:].bitcast(I32), 0)
         nc.vector.memset(w2s_d[:].bitcast(I32), 0)
         nc.vector.memset(xs1[:].bitcast(I32), 0)
+        nc.vector.memset(w3s1[:].bitcast(I32), 0)
 
         def load_x(o):
             nc.sync.dma_start(xw[o][:], x_words[o].rearrange("p n t -> p (n t)").bitcast(I32))
@@ -91,7 +93,7 @@ def tile_picked_zskip_relu_po_kernel(
 
         def load_w3_scales(r):
             nc.sync.dma_start(
-                w3s_raw[r:P:32, :, :].bitcast(I32), w3_scales[:, r:16:4, :].rearrange("o q n -> q o n").bitcast(I32)
+                w3s_raw[r:P:16, :].bitcast(I32), w3_scales[:, r:16:4, :].rearrange("o q n -> q o n").bitcast(I32)
             )
 
         nc.scalar.activation(zero_bias[:], zero[:], ACT.Relu)
@@ -131,8 +133,8 @@ def tile_picked_zskip_relu_po_kernel(
 
         def deal_w3s():
             nc.vector.tensor_copy(
-                w3s_d[:].rearrange("p o (t m) -> p o t m", t=PACK),
-                w3s_raw[:].rearrange("p o (m t) -> p o t m", t=PACK),
+                w3s_d[:].rearrange("p (t m) -> p t m", t=PACK),
+                w3s_raw[:].rearrange("p (m t) -> p t m", t=PACK),
             )
 
         def warm(n):
@@ -183,7 +185,7 @@ def tile_picked_zskip_relu_po_kernel(
                 nc.tensor.matmul_mx(
                     out=y_ps[c][:, t, :],
                     lhsT=w3_d[o][:, 256 * t : 256 * (t + 1)].bitcast(FP4X4),
-                    lhsT_scale=w3s_d[:, o, cols(t)],
+                    lhsT_scale=(w3s_d if o == 0 else w3s1)[:, cols(t)],
                     rhs=picked(o, CHUNK * c, CHUNK * (c + 1)).bitcast(FP8X4),
                     rhs_scale=x_scale[:, cols(c)],
                     start=(o == 0 and t == 0),
@@ -256,7 +258,7 @@ def tile_picked_zskip_relu_po_kernel(
         load_w1(0)
         for r in range(4):
             load_w3_scales(r)
-        nc.sync.dma_start(w3s_raw[16:32, 0, :].bitcast(I32), w2_scales[0].bitcast(I32))
+        nc.sync.dma_start(w3s_raw[4:P:8, :].bitcast(I32), w2_scales[0].bitcast(I32))
         load_w1(1)
         deal_words(nc.vector, w3_d[0], w3_raw[0])
         gather_x(0, 0, CHUNK)
@@ -269,11 +271,12 @@ def tile_picked_zskip_relu_po_kernel(
         gather_x(0, CHUNK, S)
         deal_w3s()
         cast_w1(0, 0, 2, 0, 128, False)
-        cast_w1(0, 2, 4, 0, 48, False)
-        cast_w1(0, 2, 4, 48, 128, True)
+        cast_w1(0, 2, 4, 0, 24, False)
+        cast_w1(0, 2, 4, 24, 128, True)
+        nc.sync.dma_start(w3s1[0 : P - 16, :].bitcast(I32), w3s_d[16:P, :].bitcast(I32))
         for q in range(4):
             nc.sync.dma_start(
-                w2s_d[32 * q : 32 * q + 4, :].bitcast(I32), w3s_d[16 + 4 * q : 20 + 4 * q, 0, :].bitcast(I32)
+                w2s_d[32 * q : 32 * q + 4, :].bitcast(I32), w3s_d[32 * q + 4 : 32 * q + 32 : 8, :].bitcast(I32)
             )
         for c in range(CHUNKS):
             mm3(0, c)

@@ -120,7 +120,7 @@ def tile_picked_zskip_relu_po_kernel(
                 )
 
         def deal_words(engine, dealt, raw):
-            engine.tensor_copy(
+            engine(
                 dealt[:].bitcast(U16).rearrange("p (t m) -> p t m", t=PACK),
                 raw[:].bitcast(U16).rearrange("p (m t) -> p t m", t=PACK),
             )
@@ -252,15 +252,15 @@ def tile_picked_zskip_relu_po_kernel(
                 queue = nc.sync if q < 2 else nc.scalar
                 queue.dma_start(out_2[0, 4 * q : 4 * q + 4, :].bitcast(I32), y_s[32 * q : 32 * q + 4, :].bitcast(I32))
 
-        load_w3(0)
         load_x(0)
         load_x_scales()
+        load_w3(0)
         load_w1(0)
         for r in range(4):
             load_w3_scales(r)
         nc.sync.dma_start(w3s_raw[4:P:8, :].bitcast(I32), w2_scales[0].bitcast(I32))
         load_w1(1)
-        deal_words(nc.vector, w3_d[0], w3_raw[0])
+        deal_words(nc.scalar.copy, w3_d[0], w3_raw[0])
         gather_x(0, 0, CHUNK)
         warm(4)
         gather_scales()
@@ -269,10 +269,11 @@ def tile_picked_zskip_relu_po_kernel(
         load_w3(1)
         load_w2()
         gather_x(0, CHUNK, S)
+        cast_w1(0, 0, 2, 0, 80, False)
+        cast_w1(0, 0, 2, 80, 128, True)
         deal_w3s()
-        cast_w1(0, 0, 2, 0, 128, False)
-        cast_w1(0, 2, 4, 0, 24, False)
-        cast_w1(0, 2, 4, 24, 128, True)
+        cast_w1(0, 2, 4, 0, 56, False)
+        cast_w1(0, 2, 4, 56, 128, True)
         nc.sync.dma_start(w3s1[0 : P - 16, :].bitcast(I32), w3s_d[16:P, :].bitcast(I32))
         for q in range(4):
             nc.sync.dma_start(
@@ -291,8 +292,8 @@ def tile_picked_zskip_relu_po_kernel(
         quant_w1(1, 2, 4)
         for c in range(1, CHUNKS):
             gather_x(1, CHUNK * c, CHUNK * (c + 1))
-        deal_words(nc.gpsimd, w3_d[1], w3_raw[1])
-        deal_words(nc.gpsimd, w2_d, w2_raw)
+        deal_words(nc.gpsimd.tensor_copy, w3_d[1], w3_raw[1])
+        deal_words(nc.gpsimd.tensor_copy, w2_d, w2_raw)
         mm1(1, 0)
         relu_h(0, False)
         quant_h(0)

@@ -30,7 +30,6 @@ def tile_picked_zskip_relu_po_kernel(
     with ExitStack() as ctx:
         sb = ctx.enter_context(tc.tile_pool(name="sb", bufs=1))
         reused = ctx.enter_context(tc.tile_pool(name="reused", bufs=1))
-        late = ctx.enter_context(tc.tile_pool(name="late", bufs=1))
         ps = ctx.enter_context(tc.psum_pool(name="ps", bufs=1))
 
         def tile(shape, dtype, name, tag=None):
@@ -58,18 +57,20 @@ def tile_picked_zskip_relu_po_kernel(
             ],
             [
                 tile([P, 2, P, PACK], BF16, "w1_bf10"),
-                late.tile([P, 2, P, PACK], BF16, name="w1_bf11", offset=0, align_bytes=256),
+                tile([P, 2, P, PACK], BF16, "w1_bf11"),
             ],
         ]
-        w3_d = [tile([P, 2 * N], U8, "w3_d0"), late.tile([P, 2 * N], U8, name="w3_d1", offset=0, align_bytes=256)]
-        w2_d = late.tile([P, 2 * N], U8, name="w2_d", offset=2 * N, align_bytes=256)
+        w3_d = [tile([P, 2 * N], U8, "w3_d0"), tile([P, 2 * N], U8, "w3_d1")]
+        w2_d = tile([P, 2 * N], U8, "w2_d")
         w1_q = [tile([P, H], U32, f"w1_q{o}") for o in range(PASSES)]
         w1_s = [reused.tile([P, H], U8, name="w1_s0", offset=0, align_bytes=256), tile([P, H], U8, "w1_s1")]
         h_bf = [tile([P, CHUNK, PACK], BF16, f"h_bf{c}") for c in range(CHUNKS)]
         h_q = [tile([P, CHUNK], U32, f"h_q{c}") for c in range(CHUNKS)]
         h_s = [tile([P, CHUNK], U8, f"h_s{c}") for c in range(CHUNKS)]
         y = [tile([P, PACK, CHUNK], F32, f"y{c}") for c in range(CHUNKS)]
-        y_bf = [tile([P, CHUNK, PACK], BF16, f"y_bf{c}") for c in range(CHUNKS)]
+        y_bf01 = tile([P, 2 * CHUNK, PACK], BF16, "y_bf01")
+        y_bf = [y_bf01[:, 0:CHUNK, :], y_bf01[:, CHUNK : 2 * CHUNK, :]]
+        y_bf.extend(tile([P, CHUNK, PACK], BF16, f"y_bf{c}")[:] for c in range(2, CHUNKS))
         y_q = tile([P, S], U32, "y_q")
         y_s = tile([P, S], U8, "y_s")
         zero = tile([P, 1], F32, "zero")
@@ -142,9 +143,9 @@ def tile_picked_zskip_relu_po_kernel(
                 nc.tensor.matmul_mx(
                     out=h_ps[CHUNKS - 1 - i % 2][:].rearrange("p t n -> p (t n)"),
                     lhsT=xg0_first[:].bitcast(FP8X4),
-                    lhsT_scale=xs1[:, 0:CHUNK],
+                    lhsT_scale=w2s_d[:, 0:CHUNK],
                     rhs=w3_d[0][:].bitcast(FP4X4),
-                    rhs_scale=xs1[:],
+                    rhs_scale=w2s_d[:],
                     start=True,
                     stop=True,
                 )
@@ -265,9 +266,8 @@ def tile_picked_zskip_relu_po_kernel(
         warm(4)
         gather_scales()
         load_x(1)
-        move_scales()
-        load_w3(1)
         load_w2()
+        move_scales()
         gather_x(0, CHUNK, S)
         cast_w1(0, 0, 2, 0, 80, False)
         cast_w1(0, 0, 2, 80, 128, True)
@@ -276,6 +276,8 @@ def tile_picked_zskip_relu_po_kernel(
         cast_w1(0, 2, 4, 56, 128, True)
         nc.sync.dma_start(w3s1[0 : P - 16, :].bitcast(I32), w3s_d[16:P, :].bitcast(I32))
         for q in range(4):
+            if q == 3:
+                load_w3(1)
             nc.sync.dma_start(
                 w2s_d[32 * q : 32 * q + 4, :].bitcast(I32), w3s_d[32 * q + 4 : 32 * q + 32 : 8, :].bitcast(I32)
             )
@@ -293,7 +295,7 @@ def tile_picked_zskip_relu_po_kernel(
         for c in range(1, CHUNKS):
             gather_x(1, CHUNK * c, CHUNK * (c + 1))
         deal_words(nc.gpsimd.tensor_copy, w3_d[1], w3_raw[1])
-        deal_words(nc.gpsimd.tensor_copy, w2_d, w2_raw)
+        deal_words(nc.scalar.copy, w2_d, w2_raw)
         mm1(1, 0)
         relu_h(0, False)
         quant_h(0)
@@ -309,27 +311,31 @@ def tile_picked_zskip_relu_po_kernel(
         mm3(1, 0)
         mm3(1, 1)
         mm2(0, True)
+        mm2(1, True)
+        mm3(1, 2)
+        mm2(2, True)
+        mm3(1, 3)
+        mm2(3, True)
         for t0 in (0, 2):
             nc.scalar.copy(y[0][:, t0 : t0 + 2, :], y_ps[0][:, t0 : t0 + 2, :])
             nc.sync.dma_start(out_rows[:, t0 : t0 + 2, cols(0)], y[0][:, t0 : t0 + 2, :])
         round_y(0, 0, 128)
-        quant_y(0, 0, 128)
-        mm3(1, 2)
-        mm2(1, True)
         copy_y(1, 0, 128, True)
         store_y(1)
         round_y(1, 0, 128)
-        quant_y(1, 0, 128)
-        mm2(2, True)
+        nc.vector.quantize_mx(
+            out=y_q[:, 0 : 2 * CHUNK].bitcast(FP8X4),
+            scales=y_s[:, 0 : 2 * CHUNK],
+            in_=y_bf01[:].rearrange("p n t -> p (n t)"),
+        )
         copy_y(2, 0, 128, False)
         store_y(2)
         round_y(2, 0, 128)
         quant_y(2, 0, 128)
-        mm2(3, False)
-        mm3(1, 3, True)
         copy_y(3, 0, 128, False)
         store_y(3)
-        round_y_psum(3, 0, 128)
-        quant_y(3, 0, 128)
+        for n0 in (0, 64):
+            round_y_psum(3, n0, n0 + 64)
+            quant_y(3, n0, n0 + 64)
         store_words(0, 4)
         store_scales()

@@ -143,9 +143,9 @@ def tile_picked_zskip_relu_po_kernel(
                 nc.tensor.matmul_mx(
                     out=h_ps[CHUNKS - 1 - i % 2][:].rearrange("p t n -> p (t n)"),
                     lhsT=xg0_first[:].bitcast(FP8X4),
-                    lhsT_scale=w2s_d[:, 0:CHUNK],
-                    rhs=w3_d[0][:].bitcast(FP4X4),
-                    rhs_scale=w2s_d[:],
+                    lhsT_scale=w3_raw[0][:, 0:CHUNK],
+                    rhs=w3_raw[0][:].bitcast(FP4X4),
+                    rhs_scale=w3_raw[0][:, 0:S],
                     start=True,
                     stop=True,
                 )

@@ -206,11 +206,12 @@ def tile_picked_zskip_relu_po_kernel(
                 )
 
         def relu_h(c, on_vector):
-            src = h_ps[c][:].rearrange("p t n -> p n t")
+            src = h_ps[c][:].rearrange("p t (n i) -> p n t i", i=2)
+            dst = h_bf[c][:].rearrange("p (n i) t -> p n t i", i=2)
             if on_vector:
-                nc.vector.tensor_scalar_max(h_bf[c][:], src, 0.0)
+                nc.vector.tensor_scalar_max(dst, src, 0.0)
             else:
-                nc.scalar.activation(h_bf[c][:], src, ACT.Relu, bias=zero_bias[:])
+                nc.scalar.activation(dst, src, ACT.Relu, bias=zero_bias[:])
 
         def quant_h(c):
             nc.vector.quantize_mx(
@@ -236,7 +237,10 @@ def tile_picked_zskip_relu_po_kernel(
             )
 
         def round_y_psum(c, n0, n1):
-            nc.scalar.copy(y_bf[c][:, n0:n1, :], y_ps[c][:, :, n0:n1].rearrange("p t n -> p n t"))
+            nc.scalar.copy(
+                y_bf[c][:, n0:n1, :].rearrange("p (n i) t -> p n t i", i=2),
+                y_ps[c][:, :, n0:n1].rearrange("p t (n i) -> p n t i", i=2),
+            )
 
         def quant_y(c, n0, n1):
             nc.vector.quantize_mx(

from contextlib import ExitStack

import concourse.mybir as mybir

K, T, S, H, N = 1024, 1024, 512, 512, 512
FLOPS = 2 * S * (K * H + H * N + K * N)

F32 = mybir.dt.float32
BF16 = mybir.dt.bfloat16
I32 = mybir.dt.int32
U32 = mybir.dt.uint32
U16 = mybir.dt.uint16
U8 = mybir.dt.uint8
FP8X4 = mybir.dt.float8_e4m3fn_x4
FP4X4 = mybir.dt.float4_e2m1fn_x4
ACT = mybir.ActivationFunctionType

P = 128
PACK = 4
K_PASS = P * PACK
PASSES = K // K_PASS
CHUNK = 128
CHUNKS = S // CHUNK


def tile_picked_zskip_relu_po_kernel(
    tc, x_words, x_scales, w1, w2_words, w2_scales, w3_words, w3_scales, offs, out_0, out_1, out_2
):
    nc = tc.nc
    with ExitStack() as ctx:
        sb = ctx.enter_context(tc.tile_pool(name="sb", bufs=1))
        reused = ctx.enter_context(tc.tile_pool(name="reused", bufs=1))
        ps = ctx.enter_context(tc.psum_pool(name="ps", bufs=1))

        def tile(shape, dtype, name, tag=None):
            return sb.tile(shape, dtype, name=name, tag=tag or name, align_bytes=256)

        offsets = sb.tile([P, S // 16], U16, name="offsets")
        xw = [tile([P, T], I32, f"xw{o}") for o in range(PASSES)]
        xs = tile([P, T], U8, "xs", "xs_then_xg0_rest")
        xg0_first = tile([P, CHUNK], U32, "xg0_first")
        xg0_rest = tile([P, S - CHUNK], U32, "xg0_rest", "xs_then_xg0_rest")
        xg1 = tile([P, S], U32, "xg1")
        xsg = tile([P, S], U8, "xsg")
        xs1 = tile([P, S], U8, "xs1")
        w3_raw = [tile([P, 2 * N], U8, f"w3_raw{o}") for o in range(PASSES)]
        w2_raw = tile([P, 2 * N], U8, "w2_raw")
        w3s_raw = reused.tile([P, N], U8, name="w3s_raw", offset=N // 2, align_bytes=256)
        w3s_d = tile([P, N], U8, "w3s_d")
        w3s1 = tile([P, N], U8, "w3s1")
        w2s_d = tile([P, N], U8, "w2s_d")
        w1_raw = [tile([P, PACK, H], F32, f"w1_raw{o}") for o in range(PASSES)]
        w1_bf = [
            [
                tile([P, 2, P, PACK], BF16, "w1_bf00"),
                reused.tile([P, 2, P, PACK], BF16, name="w1_bf01", offset=N, align_bytes=256),
            ],
            [
                tile([P, 2, P, PACK], BF16, "w1_bf10"),
                tile([P, 2, P, PACK], BF16, "w1_bf11"),
            ],
        ]
        w3_d = [tile([P, 2 * N], U8, "w3_d0"), tile([P, 2 * N], U8, "w3_d1")]
        w2_d = tile([P, 2 * N], U8, "w2_d")
        w1_q = [tile([P, H], U32, f"w1_q{o}") for o in range(PASSES)]
        w1_s = [reused.tile([P, H], U8, name="w1_s0", offset=0, align_bytes=256), tile([P, H], U8, "w1_s1")]
        h_bf = [tile([P, CHUNK, PACK], BF16, f"h_bf{c}") for c in range(CHUNKS)]
        h_q = [tile([P, CHUNK], U32, f"h_q{c}") for c in range(CHUNKS)]
        h_s = [tile([P, CHUNK], U8, f"h_s{c}") for c in range(CHUNKS)]
        y = [tile([P, PACK, CHUNK], F32, f"y{c}") for c in range(CHUNKS)]
        y_bf01 = tile([P, 2 * CHUNK, PACK], BF16, "y_bf01")
        y_bf = [y_bf01[:, 0:CHUNK, :], y_bf01[:, CHUNK : 2 * CHUNK, :]]
        y_bf.extend(tile([P, CHUNK, PACK], BF16, f"y_bf{c}")[:] for c in range(2, CHUNKS))
        y_q = tile([P, S], U32, "y_q")
        y_s = tile([P, S], U8, "y_s")
        zero = tile([P, 1], F32, "zero")
        zero_bias = tile([P, 1], F32, "zero_bias")
        h_ps = [ps.tile([P, PACK, CHUNK], F32, name=f"h_ps{c}") for c in range(CHUNKS)]
        y_ps = [ps.tile([P, PACK, CHUNK], F32, name=f"y_ps{c}") for c in range(CHUNKS)]

        nc.vector.memset(xs[:].bitcast(I32), 0)
        nc.vector.memset(zero[:], 0.0)
        nc.vector.memset(w3s_raw[:].bitcast(I32), 0)
        nc.vector.memset(w2s_d[:].bitcast(I32), 0)
        nc.vector.memset(xs1[:].bitcast(I32), 0)
        nc.vector.memset(w3s1[:].bitcast(I32), 0)

        def load_x(o):
            nc.sync.dma_start(xw[o][:], x_words[o].rearrange("p n t -> p (n t)").bitcast(I32))

        def load_w1(o):
            rows = w1[K_PASS * o : K_PASS * (o + 1), :]
            nc.sync.dma_start(w1_raw[o][:], rows.rearrange("(p j) c -> p j c", j=PACK))

        def load_w3_scales(r):
            nc.sync.dma_start(
                w3s_raw[r:P:16, :].bitcast(I32), w3_scales[:, r:16:4, :].rearrange("o q n -> q o n").bitcast(I32)
            )

        nc.scalar.activation(zero_bias[:], zero[:], ACT.Relu)

        def picked(o, n0, n1):
            if o == 1:
                return xg1[:, n0:n1]
            return xg0_first[:, n0:n1] if n1 <= CHUNK else xg0_rest[:, n0 - CHUNK : n1 - CHUNK]

        def gather_x(o, n0, n1):
            nc.vector.tensor_copy(picked(o, n0, n1), xw[o][:].bitcast(U32).indirect(offsets[:, n0 // 16 : n1 // 16]))

        def load_w2():
            nc.sync.dma_start(w2_raw[:].bitcast(I32), w2_words[0].bitcast(I32))

        def load_w3(o):
            nc.sync.dma_start(w3_raw[o][:].bitcast(I32), w3_words[o].bitcast(I32))

        def load_x_scales():
            nc.sync.dma_start(offsets[:], offs)
            for r in range(4):
                nc.sync.dma_start(
                    xs[r:P:16, :].bitcast(I32), x_scales[:, r:16:4, :].rearrange("o q n -> q o n").bitcast(I32)
                )

        def deal_words(engine, dealt, raw):
            engine(
                dealt[:].bitcast(U16).rearrange("p (t m) -> p t m", t=PACK),
                raw[:].bitcast(U16).rearrange("p (m t) -> p t m", t=PACK),
            )

        def gather_scales():
            nc.vector.tensor_copy(xsg[:], xs[:].indirect(offsets[:]))

        def move_scales():
            nc.sync.dma_start(xs1[0 : P - 16, :].bitcast(I32), xsg[16:P, :].bitcast(I32))

        def deal_w3s():
            nc.vector.tensor_copy(
                w3s_d[:].rearrange("p (t m) -> p t m", t=PACK),
                w3s_raw[:].rearrange("p (m t) -> p t m", t=PACK),
            )

        def warm(n):
            for i in range(n):
                nc.tensor.matmul_mx(
                    out=h_ps[CHUNKS - 1 - i % 2][:].rearrange("p t n -> p (t n)"),
                    lhsT=xg0_first[:].bitcast(FP8X4),
                    lhsT_scale=w3_raw[0][:, 0:CHUNK],
                    rhs=w3_raw[0][:].bitcast(FP4X4),
                    rhs_scale=w3_raw[0][:, 0:S],
                    start=True,
                    stop=True,
                )

        def cast_w1(o, t0, t1, m0, m1, on_vector):
            dst = w1_bf[o][t0 // 2][:, :, m0:m1, :].rearrange("p t m j -> p m j t")
            src = w1_raw[o][:].rearrange("p j (m t) -> p m j t", t=PACK)[:, m0:m1, :, t0:t1]
            if on_vector:
                nc.vector.tensor_copy(dst, src)
            else:
                nc.scalar.activation(dst, src, ACT.Copy)

        def quant_w1(o, t0, t1):
            nc.vector.quantize_mx(
                out=w1_q[o][:, P * t0 : P * t1].bitcast(FP8X4),
                scales=w1_s[o][:, P * t0 : P * t1],
                in_=w1_bf[o][t0 // 2][:].rearrange("p t m j -> p (t m j)"),
            )

        def cols(i):
            return slice(P * i, P * (i + 1))

        def mm1(o, c):
            for t in range(PACK):
                nc.tensor.matmul_mx(
                    out=h_ps[c][:, t, :],
                    lhsT=w1_q[o][:, cols(t)].bitcast(FP8X4),
                    lhsT_scale=w1_s[o][:, cols(t)],
                    rhs=picked(o, CHUNK * c, CHUNK * (c + 1)).bitcast(FP8X4),
                    rhs_scale=(xsg if o == 0 else xs1)[:, cols(c)],
                    start=(o == 0 and t == 0),
                    stop=(o == PASSES - 1 and t == PACK - 1),
                )

        def mm3(o, c, last=False):
            x_scale = xsg if o == 0 else xs1
            for t in range(PACK):
                nc.tensor.matmul_mx(
                    out=y_ps[c][:, t, :],
                    lhsT=w3_d[o][:, 256 * t : 256 * (t + 1)].bitcast(FP4X4),
                    lhsT_scale=(w3s_d if o == 0 else w3s1)[:, cols(t)],
                    rhs=picked(o, CHUNK * c, CHUNK * (c + 1)).bitcast(FP8X4),
                    rhs_scale=x_scale[:, cols(c)],
                    start=(o == 0 and t == 0),
                    stop=(last and t == PACK - 1),
                )

        def mm2(c, last):
            for t in range(PACK):
                nc.tensor.matmul_mx(
                    out=y_ps[c][:, t, :],
                    lhsT=w2_d[:, 256 * t : 256 * (t + 1)].bitcast(FP4X4),
                    lhsT_scale=w2s_d[:, cols(t)],
                    rhs=h_q[c][:].bitcast(FP8X4),
                    rhs_scale=h_s[c][:],
                    start=False,
                    stop=(last and t == PACK - 1),
                )

        def relu_h(c, on_vector):
            src = h_ps[c][:].rearrange("p t (n i) -> p n t i", i=2)
            dst = h_bf[c][:].rearrange("p (n i) t -> p n t i", i=2)
            if on_vector:
                nc.vector.tensor_scalar_max(dst, src, 0.0)
            else:
                nc.scalar.activation(dst, src, ACT.Relu, bias=zero_bias[:])

        def quant_h(c):
            nc.vector.quantize_mx(
                out=h_q[c][:].bitcast(FP8X4), scales=h_s[c][:], in_=h_bf[c][:].rearrange("p n t -> p (n t)")
            )

        out_rows = out_0.rearrange("(p t) n -> p t n", t=PACK)
        out_words = out_1[0].rearrange("p n t -> p (n t)").bitcast(I32)

        def copy_y(c, n0, n1, on_vector):
            if on_vector:
                nc.vector.tensor_copy(y[c][:, :, n0:n1], y_ps[c][:, :, n0:n1])
            else:
                nc.scalar.copy(y[c][:, :, n0:n1], y_ps[c][:, :, n0:n1])

        def store_y(c):
            nc.sync.dma_start(out_rows[:, :, cols(c)], y[c][:])

        def round_y(c, n0, n1):
            nc.vector.tensor_copy(
                y_bf[c][:, n0:n1, :].rearrange("p (n i) t -> p n t i", i=4),
                y[c][:, :, n0:n1].rearrange("p t (n i) -> p n t i", i=4),
            )

        def round_y_psum(c, n0, n1):
            nc.scalar.copy(
                y_bf[c][:, n0:n1, :].rearrange("p (n i) t -> p n t i", i=2),
                y_ps[c][:, :, n0:n1].rearrange("p t (n i) -> p n t i", i=2),
            )

        def quant_y(c, n0, n1):
            nc.vector.quantize_mx(
                out=y_q[:, CHUNK * c + n0 : CHUNK * c + n1].bitcast(FP8X4),
                scales=y_s[:, CHUNK * c + n0 : CHUNK * c + n1],
                in_=y_bf[c][:, n0:n1, :].rearrange("p n t -> p (n t)"),
            )

        def store_words(c0, c1):
            nc.sync.dma_start(out_words[:, CHUNK * c0 : CHUNK * c1], y_q[:, CHUNK * c0 : CHUNK * c1].bitcast(I32))

        def store_scales():
            for q in range(4):
                queue = nc.sync if q < 2 else nc.scalar
                queue.dma_start(out_2[0, 4 * q : 4 * q + 4, :].bitcast(I32), y_s[32 * q : 32 * q + 4, :].bitcast(I32))

        load_x(0)
        load_x_scales()
        load_w3(0)
        load_w1(0)
        for r in range(4):
            load_w3_scales(r)
        nc.sync.dma_start(w3s_raw[4:P:8, :].bitcast(I32), w2_scales[0].bitcast(I32))
        load_w1(1)
        deal_words(nc.scalar.copy, w3_d[0], w3_raw[0])
        gather_x(0, 0, CHUNK)
        warm(4)
        gather_scales()
        load_x(1)
        load_w2()
        move_scales()
        gather_x(0, CHUNK, S)
        cast_w1(0, 0, 2, 0, 80, False)
        cast_w1(0, 0, 2, 80, 128, True)
        deal_w3s()
        cast_w1(0, 2, 4, 0, 56, False)
        cast_w1(0, 2, 4, 56, 128, True)
        nc.sync.dma_start(w3s1[0 : P - 16, :].bitcast(I32), w3s_d[16:P, :].bitcast(I32))
        for q in range(4):
            if q == 3:
                load_w3(1)
            nc.sync.dma_start(
                w2s_d[32 * q : 32 * q + 4, :].bitcast(I32), w3s_d[32 * q + 4 : 32 * q + 32 : 8, :].bitcast(I32)
            )
        for c in range(CHUNKS):
            mm3(0, c)
        quant_w1(0, 0, 2)
        quant_w1(0, 2, 4)
        for c in range(CHUNKS):
            mm1(0, c)
        cast_w1(1, 2, 4, 0, 128, False)
        cast_w1(1, 0, 2, 0, 128, True)
        quant_w1(1, 0, 2)
        gather_x(1, 0, CHUNK)
        quant_w1(1, 2, 4)
        for c in range(1, CHUNKS):
            gather_x(1, CHUNK * c, CHUNK * (c + 1))
        deal_words(nc.gpsimd.tensor_copy, w3_d[1], w3_raw[1])
        deal_words(nc.scalar.copy, w2_d, w2_raw)
        mm1(1, 0)
        relu_h(0, False)
        quant_h(0)
        mm1(1, 1)
        relu_h(1, True)
        quant_h(1)
        mm1(1, 2)
        relu_h(2, False)
        quant_h(2)
        mm1(1, 3)
        relu_h(3, False)
        quant_h(3)
        mm3(1, 0)
        mm3(1, 1)
        mm2(0, True)
        mm2(1, True)
        mm3(1, 2)
        mm2(2, True)
        mm3(1, 3)
        mm2(3, True)
        for t0 in (0, 2):
            nc.scalar.copy(y[0][:, t0 : t0 + 2, :], y_ps[0][:, t0 : t0 + 2, :])
            nc.sync.dma_start(out_rows[:, t0 : t0 + 2, cols(0)], y[0][:, t0 : t0 + 2, :])
        round_y(0, 0, 128)
        copy_y(1, 0, 128, True)
        store_y(1)
        round_y(1, 0, 128)
        nc.vector.quantize_mx(
            out=y_q[:, 0 : 2 * CHUNK].bitcast(FP8X4),
            scales=y_s[:, 0 : 2 * CHUNK],
            in_=y_bf01[:].rearrange("p n t -> p (n t)"),
        )
        copy_y(2, 0, 128, False)
        store_y(2)
        round_y(2, 0, 128)
        quant_y(2, 0, 128)
        copy_y(3, 0, 128, False)
        store_y(3)
        for n0 in (0, 64):
            round_y_psum(3, n0, n0 + 64)
            quant_y(3, n0, n0 + 64)
        store_words(0, 4)
        store_scales()
